import numpy as np
import ml_dtypes


def mxq(x, axis, fmt="e4m3"):
    dtype, down = {"e4m3": (ml_dtypes.float8_e4m3fn, 7), "e5m2": (ml_dtypes.float8_e5m2, 14)}[fmt]
    v = np.moveaxis(np.asarray(x, np.float32).astype(ml_dtypes.bfloat16).astype(np.float64), axis, -1)
    blocks = v.reshape(v.shape[:-1] + (-1, 32))
    amax = np.abs(blocks).max(-1, keepdims=True)
    byte = np.maximum(np.where(amax > 0, np.frexp(amax)[1] - 1 + 127, 0) - down, 1)
    scale = np.exp2(byte - 127.0)
    codes = (blocks / scale).astype(np.float32).astype(dtype).astype(np.float64)
    return np.moveaxis((codes * scale).reshape(v.shape), -1, axis)


WIDE = False


def mx_kscale(k):
    if not WIDE:
        return np.ones(k)
    levels = np.array([10, -10, 5, -5, 0])
    if k % 512:
        return np.exp2(np.random.permutation(np.resize(levels, k // 32))).repeat(32)
    a = np.empty((k // 512, 16))
    for p in range(k // 512):
        a[p, :8] = np.random.permutation(np.resize(levels, 8))
        for g in range(8):
            far = levels[np.abs(levels - a[p, g]) >= 10]
            a[p, g + 8] = far[np.random.randint(len(far))]
    return np.exp2(a.ravel()).repeat(32)


def f64(x):
    return np.asarray(x).astype(np.float64)


def striped(idx):
    return np.tile(idx.reshape(-1, 16).T, (8, 1)).astype(np.uint16)


def unstriped(offs):
    return offs[:16].T.reshape(-1).astype(np.int64)


E2M1 = np.array([0.0, 0.5, 1.0, 1.5, 2.0, 3.0, 4.0, 6.0, -0.0, -0.5, -1.0, -1.5, -2.0, -3.0, -4.0, -6.0])


def pack_weight(w, fmt):
    k, n = w.shape
    w = f64(np.asarray(w, np.float32).astype(ml_dtypes.bfloat16)).reshape(k // 32, 32, n)
    amax = np.abs(w).max(1)
    if fmt == "e4m3":
        byte = np.frexp(amax)[1] - 1 + 127 - 7
    else:
        mant, ex = np.frexp(amax / 6.0)
        byte = np.where(mant > 0.5, ex, ex - 1) + 127
    byte = np.clip(np.where(amax > 0, byte, 1), 1, 254)
    scaled = (w * np.exp2(127.0 - byte)[:, None, :]).reshape(k, n).astype(np.float32)
    by_word = np.ascontiguousarray(scaled.reshape(k // 512, 128, 4, n).transpose(0, 1, 3, 2))
    if fmt == "e4m3":
        words = by_word.astype(ml_dtypes.float8_e4m3fn).view(np.uint8)
    else:
        c = by_word.astype(ml_dtypes.float4_e2m1fn).view(np.uint8) & 0xF
        words = (c[..., 0::2] | (c[..., 1::2] << 4)).reshape(k // 512, 128, 2 * n)
    return np.ascontiguousarray(words), np.ascontiguousarray(byte.astype(np.uint8).reshape(k // 512, 16, n))


def unpack_weight(words, scales, fmt):
    g, _, n = scales.shape
    words = np.ascontiguousarray(words).reshape(g, 128, n, -1)
    if fmt == "e4m3":
        vals = words.view(ml_dtypes.float8_e4m3fn).astype(np.float64)
    else:
        nib = np.empty((g, 128, n, 4), np.uint8)
        nib[..., 0::2] = words & 0xF
        nib[..., 1::2] = words >> 4
        vals = E2M1[nib]
    vals = vals * np.repeat(np.exp2(scales.astype(np.float64) - 127.0), 8, axis=1)[..., None]
    return vals.transpose(0, 1, 3, 2).reshape(g * 512, n)


def gelu(v):
    return 0.5 * v * (1.0 + np.tanh(np.sqrt(2.0 / np.pi) * (v + 0.044715 * v**3)))


def bf(x):
    return np.asarray(x, np.float32).astype(ml_dtypes.bfloat16)


def planes(Y):
    n, m = Y.shape
    b = f64(bf(Y)).reshape(n // 32, 32, m)
    amax = np.abs(b).max(1)
    byte = np.clip(np.where(amax > 0, np.frexp(amax)[1] - 1 + 127 - 7, 1), 1, 254)
    codes = (b * np.exp2(127.0 - byte)[:, None, :]).reshape(n, m).astype(np.float32).astype(ml_dtypes.float8_e4m3fn).view(np.uint8)
    words = codes.reshape(n // 512, 128, 4, m).transpose(0, 1, 3, 2)
    return np.ascontiguousarray(words), np.ascontiguousarray(byte.astype(np.uint8).reshape(n // 512, 16, m))


K, T, S, H, T2, P, N = 512, 4096, 1024, 1024, 2048, 1024, 512

def setup_inputs():
    n = np.random.standard_normal
    s = mx_kscale(K)[:, None]
    u = mx_kscale(H)[:, None]
    d = {}
    d["tab_words"], d["tab_scales"] = pack_weight(n((K, T)) * s, "e4m3")
    d["offs"] = striped(np.random.permutation(T)[:S])
    d["offs2"] = striped(np.random.permutation(T2)[:S])
    d["offs3"] = striped(np.random.permutation(T2)[:P])
    d["w1"] = (n((K, H)) / s * u.T / K**0.5).astype(np.float32)
    d["w2_words"], d["w2_scales"] = pack_weight(n((H, H)) / u * u.T / H**0.5, "e2m1")
    d["wgs"] = np.exp(0.3 * n((128, S))).astype(np.float32)
    d["page0"] = (n((H, T2)) * u).astype(np.float32)
    d["gm"] = n((H, P)).astype(np.float32)
    d["w4"] = (n((H, N)) / u / H**0.5).astype(np.float32)
    d["b4"] = (0.5 * n(N)).astype(np.float32)
    return d

def reference(tab_words, tab_scales, offs, offs2, offs3, w1, w2_words, w2_scales, wgs, page0, gm, w4, b4):
    v = unpack_weight(tab_words, tab_scales, "e4m3")[:, unstriped(offs)]
    w2 = unpack_weight(w2_words, w2_scales, "e2m1")
    raw = mxq(f64(w1), 0, "e4m3").T @ v
    mag = np.abs(raw)
    h = (w2.T @ mxq(mag, 0, "e4m3")) + raw
    page = f64(page0).copy()
    page[:, unstriped(offs2)] = np.tile(f64(wgs), (H // 128, 1)) * h
    x = page[:, unstriped(offs3)] * f64(gm)
    y = np.tanh((mxq(f64(w4), 0, "e4m3").T @ mxq(x, 0, "e4m3")) + f64(b4)[:, None])
    words, scales = planes(page)
    return y, page, words, scales

@@ -1,0 +1,379 @@
+from contextlib import ExitStack
+
+import concourse.mybir as mybir
+from concourse.masks import make_identity
+
+K, T, S, H, T2, PICKS, N = 512, 4096, 1024, 1024, 2048, 1024, 512
+FLOPS = 2 * (K * H * S + H * H * S + H * N * PICKS)
+
+F32 = mybir.dt.float32
+BF16 = mybir.dt.bfloat16
+I32 = mybir.dt.int32
+U32 = mybir.dt.uint32
+U16 = mybir.dt.uint16
+U8 = mybir.dt.uint8
+FP8X4 = mybir.dt.float8_e4m3fn_x4
+FP4X4 = mybir.dt.float4_e2m1fn_x4
+ACT = mybir.ActivationFunctionType
+MULT = mybir.AluOpType.mult
+ADD = mybir.AluOpType.add
+
+P = 128
+PACK = 4
+PASS = P * PACK
+GROUPS = H // PASS
+BANK = 512
+CHUNK = 128
+QUARTER = 256
+ADDED_ON_VECTOR = 5
+X_PIECES = ((0, 512), (512, 256), (768, 256))
+
+
+def tile_list_lens_slot_refresh_kernel(
+    tc, tab_words, tab_scales, offs, offs2, offs3, w1, w2_words, w2_scales, wgs, page0, gm, w4, b4,
+    out_0, out_1, out_2, out_3,
+):
+    nc = tc.nc
+    with ExitStack() as ctx:
+        lists = ctx.enter_context(tc.tile_pool(name="lists", bufs=1))
+        keep = ctx.enter_context(tc.tile_pool(name="keep", bufs=1))
+        ring = ctx.enter_context(tc.tile_pool(name="ring", bufs=2))
+        psum = ctx.enter_context(tc.psum_pool(name="psum", bufs=4))
+
+        def listed(tile, first, count):
+            return tile[:, first // 16 : (first + count) // 16]
+
+        def stage_tile(shape, dtype):
+            return ring.tile(shape, dtype, name="stage", tag="stage", bufs=3, align_bytes=64)
+
+        def rounded_tile():
+            return ring.tile([P, 2048], BF16, name="rounded", tag="rounded", bufs=3, align_bytes=64)
+
+        pick = lists.tile([P, S // 16], U16, name="pick")
+        put = lists.tile([P, S // 16], U16, name="put")
+        fetch = lists.tile([P, PICKS // 16], U16, name="fetch")
+
+        tab_s = keep.tile([P, T], U8, name="tab_s", align_bytes=64)
+        w2_s_raw = keep.tile([P, GROUPS, H], U8, name="w2_s_raw", align_bytes=64)
+        nc.vector.memset(tab_s[:].bitcast(I32), 0)
+        nc.gpsimd.memset(w2_s_raw[:].rearrange("p a c -> p (a c)").bitcast(I32), 0)
+
+        w1_rows = w1.rearrange("(p j) c -> p j c", j=PACK)
+        w1_raw = []
+        for g in range(GROUPS):
+            raw = stage_tile([P, PACK, PASS], F32)
+            nc.sync.dma_start(out=raw[:], in_=w1_rows[:, :, g * PASS : (g + 1) * PASS])
+            w1_raw.append(raw)
+            if g == 0:
+                for q in range(4):
+                    nc.sync.dma_start(
+                        out=tab_s[32 * q : 32 * q + 4, :].bitcast(I32),
+                        in_=tab_scales[0, 4 * q : 4 * q + 4, :].bitcast(I32),
+                    )
+                for q in range(4):
+                    nc.sync.dma_start(
+                        out=w2_s_raw[32 * q : 32 * q + 4, :, :].bitcast(I32),
+                        in_=w2_scales[:, 4 * q : 4 * q + 4, :].rearrange("a q c -> q a c").bitcast(I32),
+                    )
+        w2_raw = keep.tile([P, GROUPS, 2 * H], U8, name="w2_raw", align_bytes=64)
+        nc.sync.dma_start(out=w2_raw[:].bitcast(I32), in_=w2_words.rearrange("a p c -> p a c").bitcast(I32))
+        nc.sync.dma_start(out=pick[:], in_=offs)
+        tab_w = keep.tile([P, T], I32, name="tab_w", tag="tab_w", align_bytes=64)
+        nc.sync.dma_start(out=tab_w[:], in_=tab_words[0].rearrange("p m t -> p (m t)").bitcast(I32))
+        nc.sync.dma_start(out=put[:], in_=offs2)
+
+        gate = keep.tile([P, PACK, S], F32, name="gate", tag="gate", align_bytes=64)
+        wgs_rows = wgs.rearrange("(q t) j -> q t j", t=PACK)
+
+        def load_gate(half):
+            cols = slice(half * S // 2, (half + 1) * S // 2)
+            for q in (0, 2, 1, 3):
+                nc.sync.dma_start(out=gate[32 * q : 32 * q + 32, :, cols], in_=wgs_rows[:, :, cols])
+
+        page0_rows = page0.rearrange("(g p t) m -> g t p m", p=P, t=PACK)
+        out_1_rows = out_1.rearrange("(g p t) m -> g t p m", p=P, t=PACK)
+        page = {}
+
+        def load_pages(g):
+            for t in range(PACK):
+                page[g, t] = keep.tile([P, T2], F32, name="page%d%d" % (g, t))
+                nc.sync.dma_start(out=page[g, t][:], in_=page0_rows[g, t])
+
+        load_gate(0)
+        load_pages(0)
+        load_gate(1)
+        load_pages(1)
+        w4_raw = []
+        for g in range(GROUPS):
+            raw = stage_tile([P, PACK, N], F32)
+            nc.sync.dma_start(out=raw[:], in_=w4[g * PASS : (g + 1) * PASS, :].rearrange("(p j) c -> p j c", j=PACK))
+            w4_raw.append(raw)
+        nc.sync.dma_start(out=fetch[:], in_=offs3)
+        bias = keep.tile([P, PACK], F32, name="bias")
+        nc.sync.dma_start(out=bias[:], in_=b4.rearrange("(p t) -> p t", t=PACK))
+
+        ident = keep.tile([P, P], F32, name="ident")
+        make_identity(nc, ident[:])
+
+        def quantise_weight(raw, copy, codes, scales):
+            rounded = rounded_tile()
+            copy(
+                out=rounded[:].rearrange("p (t m j) -> p m j t", t=PACK, j=PACK),
+                in_=raw[:].rearrange("p j (m t) -> p m j t", t=PACK),
+            )
+            nc.vector.quantize_mx(out=codes.bitcast(FP8X4), scales=scales, in_=rounded[:])
+
+        w1_c = keep.tile([P, GROUPS, PASS], U32, name="w1_c", align_bytes=64)
+        w1_s = keep.tile([P, GROUPS, PASS], U8, name="w1_s", align_bytes=64)
+        quantise_weight(w1_raw[0], nc.vector.tensor_copy, w1_c[:, 0, :], w1_s[:, 0, :])
+        quantise_weight(w1_raw[1], nc.scalar.copy, w1_c[:, 1, :], w1_s[:, 1, :])
+
+        w2_c = keep.tile([P, PACK, GROUPS, 2 * H // PACK], U8, name="w2_c", align_bytes=64)
+        w2_s = keep.tile([P, PACK, GROUPS, H // PACK], U8, name="w2_s", align_bytes=64)
+        nc.vector.tensor_copy(
+            out=w2_s[:].rearrange("p t a q -> p t (a q)"),
+            in_=w2_s_raw[:].rearrange("p a (q t) -> p t (a q)", t=PACK),
+        )
+        nc.vector.tensor_copy(
+            out=w2_c[:].rearrange("p t a (q b) -> p t (a q) b", b=2),
+            in_=w2_raw[:].rearrange("p a (q t b) -> p t (a q) b", t=PACK, b=2),
+        )
+
+        v_c = keep.tile([P, S], U32, name="v_c", align_bytes=64)
+        v_s = keep.tile([P, S], U8, name="v_s", align_bytes=64)
+
+        def pick_scales(first, count):
+            nc.vector.tensor_copy(v_s[:, first : first + count], tab_s[:].indirect(listed(pick, first, count)))
+
+        def pick_words(first, count):
+            nc.vector.tensor_copy(
+                v_c[:, first : first + count], tab_w[:].bitcast(U32).indirect(listed(pick, first, count))
+            )
+
+        pick_scales(0, 512)
+        pick_words(0, 256)
+
+        h = [keep.tile([P, PACK, S], F32, name="h%d" % g, tag="h%d" % g, align_bytes=64) for g in range(GROUPS)]
+        raw_banks, mags = {}, {}
+
+        def raw_pass(bank, c, g, t, start):
+            cols = slice(c * CHUNK, (c + 1) * CHUNK)
+            nc.tensor.matmul_mx(
+                out=bank[:, t * CHUNK : (t + 1) * CHUNK],
+                lhsT=w1_c[:, g, t * P : (t + 1) * P].bitcast(FP8X4),
+                lhsT_scale=w1_s[:, g, t * P : (t + 1) * P],
+                rhs=v_c[:, cols].bitcast(FP8X4),
+                rhs_scale=v_s[:, cols],
+                start=start,
+                stop=True,
+            )
+
+        def first_product(c):
+            mag = ring.tile([P, GROUPS, PASS], BF16, name="mag", align_bytes=64)
+            for g in range(GROUPS):
+                bank = psum.tile([P, BANK], F32, name="left", tag="left")
+                for t in range(PACK):
+                    raw_pass(bank, c, g, t, True)
+                nc.scalar.activation(
+                    out=mag[:, g, :].rearrange("p (n t) -> p n t", t=PACK),
+                    in_=bank[:].rearrange("p (t n) -> p n t", t=PACK),
+                    func=ACT.Abs,
+                )
+                raw_banks[c, g] = bank
+            mag_c = ring.tile([P, GROUPS * CHUNK], U32, name="mag_c", bufs=3, align_bytes=64)
+            mag_s = ring.tile([P, GROUPS * CHUNK], U8, name="mag_s", bufs=3, align_bytes=64)
+            nc.vector.quantize_mx(
+                out=mag_c[:].bitcast(FP8X4), scales=mag_s[:], in_=mag[:].rearrange("p g n -> p (g n)")
+            )
+            mags[c] = (mag_c, mag_s)
+
+        def second_product(c):
+            cols = slice(c * CHUNK, (c + 1) * CHUNK)
+            mag_c, mag_s = mags[c]
+            on_vector = c < ADDED_ON_VECTOR
+            if on_vector:
+                raw_sb = ring.tile([P, GROUPS, BANK], F32, name="raw_sb", tag="f32pair")
+                for g in range(GROUPS):
+                    nc.scalar.copy(out=raw_sb[:, g, :], in_=raw_banks[c, g][:])
+            for g in range(GROUPS):
+                bank = psum.tile([P, BANK], F32, name="right", tag="right")
+                for t in range(PACK):
+                    for a in range(GROUPS):
+                        nc.tensor.matmul_mx(
+                            out=bank[:, t * CHUNK : (t + 1) * CHUNK],
+                            lhsT=w2_c[:, t, a, 2 * g * P : 2 * (g + 1) * P].bitcast(FP4X4),
+                            lhsT_scale=w2_s[:, t, a, g * P : (g + 1) * P],
+                            rhs=mag_c[:, a * CHUNK : (a + 1) * CHUNK].bitcast(FP8X4),
+                            rhs_scale=mag_s[:, a * CHUNK : (a + 1) * CHUNK],
+                            start=(a == 0),
+                            stop=(on_vector and a == GROUPS - 1),
+                        )
+                    if not on_vector:
+                        raw_pass(bank, c, g, t, False)
+                sums = bank[:].rearrange("p (t n) -> p t n", t=PACK)
+                if on_vector:
+                    nc.vector.tensor_tensor(
+                        out=h[g][:, :, cols],
+                        in0=sums,
+                        in1=raw_sb[:, g, :].rearrange("p (t n) -> p t n", t=PACK),
+                        op=ADD,
+                    )
+                else:
+                    nc.scalar.copy(out=h[g][:, :, cols], in_=sums)
+
+        def put_columns(g, t, first, count):
+            nc.vector.tensor_tensor(
+                page[g, t][:].indirect(listed(put, first, count)),
+                h[g][:, t, first : first + count],
+                gate[:, t, first : first + count],
+                MULT,
+            )
+
+        chunks = S // CHUNK
+        first_product(0)
+        first_product(1)
+        pick_words(256, 256)
+        pick_scales(512, 512)
+        pick_words(512, 512)
+        for c in range(chunks):
+            second_product(c)
+            if c + 2 < chunks:
+                first_product(c + 2)
+            if c % 2 == 1:
+                for t in range(PACK):
+                    put_columns(0, t, (c // 2) * QUARTER, QUARTER)
+
+        out_2_words = out_2.rearrange("g p m t -> g p (m t)")
+        page_s = [keep.tile([P, T2], U8, name="page_s%d" % g, align_bytes=64) for g in range(GROUPS)]
+        pairs = {}
+
+        def turn_pair(g, u):
+            pair = stage_tile([P, T2 // P, P, 2], BF16)
+            for k in range(T2 // (2 * P)):
+                bank = psum.tile([P, BANK], F32, name="left", tag="left")
+                for b in range(2):
+                    for e in range(2):
+                        nc.tensor.transpose(
+                            bank[:, (2 * b + e) * P : (2 * b + e + 1) * P],
+                            page[g, 2 * u + e][:, (2 * k + b) * P : (2 * k + b + 1) * P],
+                            ident[:],
+                        )
+                nc.scalar.copy(
+                    out=pair[:, 2 * k : 2 * k + 2, :, :],
+                    in_=bank[:].rearrange("m (b e p) -> m b p e", b=2, e=2),
+                )
+            pairs[g, u] = pair
+
+        def store_pages(g, u):
+            for e in range(2):
+                nc.sync.dma_start(out=out_1_rows[g, 2 * u + e], in_=page[g, 2 * u + e][:])
+
+        def page_planes(g):
+            words = [pairs[g, u][:].rearrange("m b p e -> m (b p e)").bitcast(F32) for u in range(2)]
+            for piece in range(T2 // BANK):
+                rounded = rounded_tile()
+                rounded_words = rounded[:].bitcast(F32)
+                for k in range(2):
+                    bank = psum.tile([P, BANK], F32, name="right", tag="right")
+                    for b in range(2):
+                        block = 4 * piece + 2 * k + b
+                        for u in range(2):
+                            nc.tensor.transpose(
+                                bank[:, (2 * b + u) * P : (2 * b + u + 1) * P],
+                                words[u][:, block * P : (block + 1) * P],
+                                ident[:],
+                            )
+                    nc.scalar.copy(
+                        out=rounded_words[:, k * BANK : (k + 1) * BANK].rearrange("p (b m u) -> p b m u", b=2, u=2),
+                        in_=bank[:].rearrange("p (b u m) -> p b m u", b=2, u=2),
+                    )
+                codes = ring.tile([P, BANK], U32, name="page_c", bufs=4, align_bytes=64)
+                nc.vector.quantize_mx(
+                    out=codes[:].bitcast(FP8X4), scales=page_s[g][:, piece * BANK : (piece + 1) * BANK], in_=rounded[:]
+                )
+                nc.sync.dma_start(
+                    out=out_2_words[g, :, piece * 4 * BANK : (piece + 1) * 4 * BANK].bitcast(I32),
+                    in_=codes[:].bitcast(I32),
+                )
+            for q in range(4):
+                nc.sync.dma_start(
+                    out=out_3[g, 4 * q : 4 * q + 4, :].bitcast(I32), in_=page_s[g][32 * q : 32 * q + 4, :].bitcast(I32)
+                )
+
+        w4_c = keep.tile([P, GROUPS, N], U32, name="w4_c", align_bytes=64)
+        w4_s = keep.tile([P, GROUPS, N], U8, name="w4_s", align_bytes=64)
+        for g in range(GROUPS):
+            quantise_weight(w4_raw[g], nc.scalar.copy, w4_c[:, g, :], w4_s[:, g, :])
+
+        gm_rows = gm.rearrange("(g p t) j -> g p t j", p=P, t=PACK)
+        factor = []
+        for g, tag in enumerate(("tab_w", "h0")):
+            tile = keep.tile([P, PACK, PICKS], F32, name="factor%d" % g, tag=tag, align_bytes=64)
+            nc.sync.dma_start(out=tile[:], in_=gm_rows[g])
+            factor.append(tile)
+
+        for u in range(2):
+            store_pages(0, u)
+            turn_pair(0, u)
+        for t in range(2):
+            put_columns(1, t, 0, S)
+        page_planes(0)
+        store_pages(1, 0)
+        turn_pair(1, 0)
+        for t in range(2, PACK):
+            put_columns(1, t, 0, S)
+        store_pages(1, 1)
+        turn_pair(1, 1)
+
+        fetched = keep.tile([P, 2, PACK * BANK], F32, name="fetched", tag="gate", align_bytes=64)
+        out_0_rows = out_0.rearrange("(p t) j -> p t j", t=PACK)
+
+        def fetch_columns(g, first, count):
+            slot = fetched[:, g, 0 : PACK * count]
+            for t in range(PACK):
+                nc.vector.tensor_tensor(
+                    slot[:, t * count : (t + 1) * count],
+                    page[g, t][:].indirect(listed(fetch, first, count)),
+                    factor[g][:, t, first : first + count],
+                    MULT,
+                )
+            rounded = rounded_tile()
+            nc.scalar.copy(
+                out=rounded[:, 0 : PACK * count].rearrange("p (c i t) -> p c t i", i=4, t=PACK),
+                in_=slot.rearrange("p (t c i) -> p c t i", i=4, t=PACK),
+            )
+            x_c = ring.tile([P, BANK], U32, name="x_c", bufs=4, align_bytes=64)
+            x_s = ring.tile([P, BANK], U8, name="x_s", bufs=4, align_bytes=64)
+            nc.vector.quantize_mx(
+                out=x_c[:, 0:count].bitcast(FP8X4), scales=x_s[:, 0:count], in_=rounded[:, 0 : PACK * count]
+            )
+            return x_c, x_s
+
+        def last_product(first, count, xs):
+            for pair in range(2):
+                y = ring.tile([P, 2, BANK], F32, name="y", tag="f32pair")
+                for e in range(2):
+                    t = 2 * pair + e
+                    bank = psum.tile([P, BANK], F32, name="left", tag="left")
+                    for g in range(GROUPS):
+                        nc.tensor.matmul_mx(
+                            out=bank[:, 0:count],
+                            lhsT=w4_c[:, g, t * P : (t + 1) * P].bitcast(FP8X4),
+                            lhsT_scale=w4_s[:, g, t * P : (t + 1) * P],
+                            rhs=xs[g][0][:, 0:count].bitcast(FP8X4),
+                            rhs_scale=xs[g][1][:, 0:count],
+                            start=(g == 0),
+                            stop=(g == GROUPS - 1),
+                        )
+                    nc.scalar.activation(
+                        out=y[:, e, 0:count], in_=bank[:, 0:count], func=ACT.Tanh, bias=bias[:, t : t + 1]
+                    )
+                nc.sync.dma_start(
+                    out=out_0_rows[:, 2 * pair : 2 * pair + 2, first : first + count], in_=y[:, :, 0:count]
+                )
+
+        for i, (first, count) in enumerate(X_PIECES):
+            xs = [fetch_columns(g, first, count) for g in range(GROUPS)]
+            last_product(first, count, xs)
+            if i == 0:
+                page_planes(1)

@@ -25,8 +25,8 @@ GROUPS = H // PASS
 BANK = 512
 CHUNK = 128
 QUARTER = 256
-ADDED_ON_VECTOR = 5
-X_PIECES = ((0, 512), (512, 256), (768, 256))
+REPEATED = 6
+X_PIECES = ((0, 512), (512, 256), (768, 128), (896, 128))
 
 
 def tile_list_lens_slot_refresh_kernel(
@@ -38,173 +38,174 @@ def tile_list_lens_slot_refresh_kernel(
         lists = ctx.enter_context(tc.tile_pool(name="lists", bufs=1))
         keep = ctx.enter_context(tc.tile_pool(name="keep", bufs=1))
         ring = ctx.enter_context(tc.tile_pool(name="ring", bufs=2))
-        psum = ctx.enter_context(tc.psum_pool(name="psum", bufs=4))
+        psum = ctx.enter_context(tc.psum_pool(name="psum", bufs=1))
+        banks = [psum.tile([P, BANK], F32, name="bank%d" % k) for k in range(8)]
+        stage = [keep.tile([P, PACK * PASS], F32, name="stage%d" % k, align_bytes=64) for k in range(3)]
+        with tc.tile_pool(name="early", bufs=1) as early:
 
-        def listed(tile, first, count):
-            return tile[:, first // 16 : (first + count) // 16]
+            def listed(tile, first, count):
+                return tile[:, first // 16 : (first + count) // 16]
 
-        def stage_tile(shape, dtype):
-            return ring.tile(shape, dtype, name="stage", tag="stage", bufs=3, align_bytes=64)
+            pick = lists.tile([P, S // 16], U16, name="pick")
+            put = lists.tile([P, S // 16], U16, name="put")
+            fetch = lists.tile([P, PICKS // 16], U16, name="fetch")
 
-        def rounded_tile():
-            return ring.tile([P, 2048], BF16, name="rounded", tag="rounded", bufs=3, align_bytes=64)
+            tab_s = early.tile([P, T], U8, name="tab_s", align_bytes=64)
+            w2_s_raw = early.tile([P, GROUPS, H], U8, name="w2_s_raw", align_bytes=64)
+            nc.vector.memset(tab_s[:].bitcast(I32), 0)
+            nc.gpsimd.memset(w2_s_raw[:].rearrange("p a c -> p (a c)").bitcast(I32), 0)
 
-        pick = lists.tile([P, S // 16], U16, name="pick")
-        put = lists.tile([P, S // 16], U16, name="put")
-        fetch = lists.tile([P, PICKS // 16], U16, name="fetch")
-
-        tab_s = keep.tile([P, T], U8, name="tab_s", align_bytes=64)
-        w2_s_raw = keep.tile([P, GROUPS, H], U8, name="w2_s_raw", align_bytes=64)
-        nc.vector.memset(tab_s[:].bitcast(I32), 0)
-        nc.gpsimd.memset(w2_s_raw[:].rearrange("p a c -> p (a c)").bitcast(I32), 0)
-
-        w1_rows = w1.rearrange("(p j) c -> p j c", j=PACK)
-        w1_raw = []
-        for g in range(GROUPS):
-            raw = stage_tile([P, PACK, PASS], F32)
-            nc.sync.dma_start(out=raw[:], in_=w1_rows[:, :, g * PASS : (g + 1) * PASS])
-            w1_raw.append(raw)
-            if g == 0:
-                for q in range(4):
-                    nc.sync.dma_start(
-                        out=tab_s[32 * q : 32 * q + 4, :].bitcast(I32),
-                        in_=tab_scales[0, 4 * q : 4 * q + 4, :].bitcast(I32),
-                    )
-                for q in range(4):
-                    nc.sync.dma_start(
-                        out=w2_s_raw[32 * q : 32 * q + 4, :, :].bitcast(I32),
-                        in_=w2_scales[:, 4 * q : 4 * q + 4, :].rearrange("a q c -> q a c").bitcast(I32),
-                    )
-        w2_raw = keep.tile([P, GROUPS, 2 * H], U8, name="w2_raw", align_bytes=64)
-        nc.sync.dma_start(out=w2_raw[:].bitcast(I32), in_=w2_words.rearrange("a p c -> p a c").bitcast(I32))
-        nc.sync.dma_start(out=pick[:], in_=offs)
-        tab_w = keep.tile([P, T], I32, name="tab_w", tag="tab_w", align_bytes=64)
-        nc.sync.dma_start(out=tab_w[:], in_=tab_words[0].rearrange("p m t -> p (m t)").bitcast(I32))
-        nc.sync.dma_start(out=put[:], in_=offs2)
-
-        gate = keep.tile([P, PACK, S], F32, name="gate", tag="gate", align_bytes=64)
-        wgs_rows = wgs.rearrange("(q t) j -> q t j", t=PACK)
-
-        def load_gate(half):
-            cols = slice(half * S // 2, (half + 1) * S // 2)
-            for q in (0, 2, 1, 3):
-                nc.sync.dma_start(out=gate[32 * q : 32 * q + 32, :, cols], in_=wgs_rows[:, :, cols])
-
-        page0_rows = page0.rearrange("(g p t) m -> g t p m", p=P, t=PACK)
-        out_1_rows = out_1.rearrange("(g p t) m -> g t p m", p=P, t=PACK)
-        page = {}
-
-        def load_pages(g):
-            for t in range(PACK):
-                page[g, t] = keep.tile([P, T2], F32, name="page%d%d" % (g, t))
-                nc.sync.dma_start(out=page[g, t][:], in_=page0_rows[g, t])
-
-        load_gate(0)
-        load_pages(0)
-        load_gate(1)
-        load_pages(1)
-        w4_raw = []
-        for g in range(GROUPS):
-            raw = stage_tile([P, PACK, N], F32)
-            nc.sync.dma_start(out=raw[:], in_=w4[g * PASS : (g + 1) * PASS, :].rearrange("(p j) c -> p j c", j=PACK))
-            w4_raw.append(raw)
-        nc.sync.dma_start(out=fetch[:], in_=offs3)
-        bias = keep.tile([P, PACK], F32, name="bias")
-        nc.sync.dma_start(out=bias[:], in_=b4.rearrange("(p t) -> p t", t=PACK))
-
-        ident = keep.tile([P, P], F32, name="ident")
-        make_identity(nc, ident[:])
-
-        def quantise_weight(raw, copy, codes, scales):
-            rounded = rounded_tile()
-            copy(
-                out=rounded[:].rearrange("p (t m j) -> p m j t", t=PACK, j=PACK),
-                in_=raw[:].rearrange("p j (m t) -> p m j t", t=PACK),
-            )
-            nc.vector.quantize_mx(out=codes.bitcast(FP8X4), scales=scales, in_=rounded[:])
-
-        w1_c = keep.tile([P, GROUPS, PASS], U32, name="w1_c", align_bytes=64)
-        w1_s = keep.tile([P, GROUPS, PASS], U8, name="w1_s", align_bytes=64)
-        quantise_weight(w1_raw[0], nc.vector.tensor_copy, w1_c[:, 0, :], w1_s[:, 0, :])
-        quantise_weight(w1_raw[1], nc.scalar.copy, w1_c[:, 1, :], w1_s[:, 1, :])
-
-        w2_c = keep.tile([P, PACK, GROUPS, 2 * H // PACK], U8, name="w2_c", align_bytes=64)
-        w2_s = keep.tile([P, PACK, GROUPS, H // PACK], U8, name="w2_s", align_bytes=64)
-        nc.vector.tensor_copy(
-            out=w2_s[:].rearrange("p t a q -> p t (a q)"),
-            in_=w2_s_raw[:].rearrange("p a (q t) -> p t (a q)", t=PACK),
-        )
-        nc.vector.tensor_copy(
-            out=w2_c[:].rearrange("p t a (q b) -> p t (a q) b", b=2),
-            in_=w2_raw[:].rearrange("p a (q t b) -> p t (a q) b", t=PACK, b=2),
-        )
-
-        v_c = keep.tile([P, S], U32, name="v_c", align_bytes=64)
-        v_s = keep.tile([P, S], U8, name="v_s", align_bytes=64)
-
-        def pick_scales(first, count):
-            nc.vector.tensor_copy(v_s[:, first : first + count], tab_s[:].indirect(listed(pick, first, count)))
-
-        def pick_words(first, count):
-            nc.vector.tensor_copy(
-                v_c[:, first : first + count], tab_w[:].bitcast(U32).indirect(listed(pick, first, count))
-            )
-
-        pick_scales(0, 512)
-        pick_words(0, 256)
-
-        h = [keep.tile([P, PACK, S], F32, name="h%d" % g, tag="h%d" % g, align_bytes=64) for g in range(GROUPS)]
-        raw_banks, mags = {}, {}
-
-        def raw_pass(bank, c, g, t, start):
-            cols = slice(c * CHUNK, (c + 1) * CHUNK)
-            nc.tensor.matmul_mx(
-                out=bank[:, t * CHUNK : (t + 1) * CHUNK],
-                lhsT=w1_c[:, g, t * P : (t + 1) * P].bitcast(FP8X4),
-                lhsT_scale=w1_s[:, g, t * P : (t + 1) * P],
-                rhs=v_c[:, cols].bitcast(FP8X4),
-                rhs_scale=v_s[:, cols],
-                start=start,
-                stop=True,
-            )
-
-        def first_product(c):
-            mag = ring.tile([P, GROUPS, PASS], BF16, name="mag", align_bytes=64)
+            w1_rows = w1.rearrange("(p j) c -> p j c", j=PACK)
+            w1_raw = []
             for g in range(GROUPS):
-                bank = psum.tile([P, BANK], F32, name="left", tag="left")
-                for t in range(PACK):
-                    raw_pass(bank, c, g, t, True)
-                nc.scalar.activation(
-                    out=mag[:, g, :].rearrange("p (n t) -> p n t", t=PACK),
-                    in_=bank[:].rearrange("p (t n) -> p n t", t=PACK),
-                    func=ACT.Abs,
+                raw = stage[g][:].rearrange("p (j c) -> p j c", j=PACK)
+                nc.sync.dma_start(out=raw, in_=w1_rows[:, :, g * PASS : (g + 1) * PASS])
+                w1_raw.append(raw)
+                if g == 0:
+                    for q in (0, 2, 1, 3):
+                        nc.sync.dma_start(
+                            out=tab_s[32 * q : 32 * q + 4, :].bitcast(I32),
+                            in_=tab_scales[0, 4 * q : 4 * q + 4, :].bitcast(I32),
+                        )
+                    for q in (0, 2, 1, 3):
+                        nc.sync.dma_start(
+                            out=w2_s_raw[32 * q : 32 * q + 4, :, :].bitcast(I32),
+                            in_=w2_scales[:, 4 * q : 4 * q + 4, :].rearrange("a q c -> q a c").bitcast(I32),
+                        )
+            nc.sync.dma_start(out=pick[:], in_=offs)
+            tab_w = keep.tile([P, T], I32, name="tab_w", tag="tab_w", align_bytes=64)
+            nc.sync.dma_start(out=tab_w[:], in_=tab_words[0].rearrange("p m t -> p (m t)").bitcast(I32))
+            w2_raw = early.tile([P, GROUPS, 2 * H], U8, name="w2_raw", align_bytes=64)
+            nc.sync.dma_start(out=w2_raw[:].bitcast(I32), in_=w2_words.rearrange("a p c -> p a c").bitcast(I32))
+            nc.sync.dma_start(out=put[:], in_=offs2)
+
+            gate = keep.tile([P, PACK, S], F32, name="gate", tag="gate", align_bytes=64)
+            wgs_rows = wgs.rearrange("(q t) j -> q t j", t=PACK)
+
+            def load_gate(u, first, count):
+                rows, cols = slice(2 * u, 2 * u + 2), slice(first, first + count)
+                for q in (0, 2, 1, 3):
+                    nc.sync.dma_start(out=gate[32 * q : 32 * q + 32, rows, cols], in_=wgs_rows[:, rows, cols])
+
+            page0_rows = page0.rearrange("(g p t) m -> g t p m", p=P, t=PACK)
+            out_1_rows = out_1.rearrange("(g p t) m -> g t p m", p=P, t=PACK)
+            page = {}
+
+            def load_pages(g, u):
+                for t in (2 * u, 2 * u + 1):
+                    page[g, t] = keep.tile([P, T2], F32, name="page%d%d" % (g, t))
+                    nc.sync.dma_start(out=page[g, t][:], in_=page0_rows[g, t])
+
+            load_gate(0, 0, QUARTER)
+            load_pages(0, 0)
+            load_gate(0, QUARTER, S - QUARTER)
+            load_gate(1, 0, S)
+            load_pages(0, 1)
+            load_pages(1, 0)
+            load_pages(1, 1)
+            ident = keep.tile([P, P], F32, name="ident")
+            make_identity(nc, ident[:])
+
+            def quantise_weight(raw, copy, rounded, codes, scales):
+                copy(
+                    out=rounded[:].rearrange("p (t m j) -> p m j t", t=PACK, j=PACK),
+                    in_=raw.rearrange("p j (m t) -> p m j t", t=PACK),
                 )
-                raw_banks[c, g] = bank
-            mag_c = ring.tile([P, GROUPS * CHUNK], U32, name="mag_c", bufs=3, align_bytes=64)
-            mag_s = ring.tile([P, GROUPS * CHUNK], U8, name="mag_s", bufs=3, align_bytes=64)
-            nc.vector.quantize_mx(
-                out=mag_c[:].bitcast(FP8X4), scales=mag_s[:], in_=mag[:].rearrange("p g n -> p (g n)")
-            )
-            mags[c] = (mag_c, mag_s)
+                nc.vector.quantize_mx(out=codes.bitcast(FP8X4), scales=scales, in_=rounded[:])
 
-        def second_product(c):
-            cols = slice(c * CHUNK, (c + 1) * CHUNK)
-            mag_c, mag_s = mags[c]
-            on_vector = c < ADDED_ON_VECTOR
-            if on_vector:
-                raw_sb = ring.tile([P, GROUPS, BANK], F32, name="raw_sb", tag="f32pair")
-                for g in range(GROUPS):
-                    nc.scalar.copy(out=raw_sb[:, g, :], in_=raw_banks[c, g][:])
+            w1_c = early.tile([P, GROUPS, PASS], U32, name="w1_c", align_bytes=64)
+            w1_s = early.tile([P, GROUPS, PASS], U8, name="w1_s", align_bytes=64)
+            for g, copy in enumerate((nc.vector.tensor_copy, nc.scalar.copy)):
+                rounded = early.tile([P, PACK * PASS], BF16, name="w1_rounded", bufs=2, align_bytes=64)
+                quantise_weight(w1_raw[g], copy, rounded, w1_c[:, g, :], w1_s[:, g, :])
+
+            w4_raw = []
             for g in range(GROUPS):
-                bank = psum.tile([P, BANK], F32, name="right", tag="right")
+                raw = stage[(2 + g) % 3][:].rearrange("p (j c) -> p j c", j=PACK)
+                nc.sync.dma_start(out=raw, in_=w4[g * PASS : (g + 1) * PASS, :].rearrange("(p j) c -> p j c", j=PACK))
+                w4_raw.append(raw)
+            nc.sync.dma_start(out=fetch[:], in_=offs3)
+            bias = keep.tile([P, PACK], F32, name="bias")
+            nc.sync.dma_start(out=bias[:], in_=b4.rearrange("(p t) -> p t", t=PACK))
+
+            w2_c = early.tile([P, GROUPS, PACK, GROUPS, 2 * P], U8, name="w2_c", align_bytes=64)
+            w2_s = early.tile([P, PACK, GROUPS, H // PACK], U8, name="w2_s", align_bytes=64)
+            nc.vector.tensor_copy(
+                out=w2_s[:].rearrange("p t a q -> p t (a q)"),
+                in_=w2_s_raw[:].rearrange("p a (q t) -> p t (a q)", t=PACK),
+            )
+
+            def deal_w2(g):
+                nc.scalar.copy(
+                    out=w2_c[:, g, :, :, :].bitcast(U16),
+                    in_=w2_raw[:].bitcast(U16).rearrange("p a (g q t) -> p g t a q", g=GROUPS, t=PACK)[:, g, :, :, :],
+                )
+
+            deal_w2(0)
+
+            v_c = early.tile([P, S], U32, name="v_c", align_bytes=64)
+            v_s = early.tile([P, S], U8, name="v_s", align_bytes=64)
+
+            def pick_scales(first, count):
+                nc.vector.tensor_copy(v_s[:, first : first + count], tab_s[:].indirect(listed(pick, first, count)))
+
+            def pick_words(first, count):
+                nc.vector.tensor_copy(
+                    v_c[:, first : first + count], tab_w[:].bitcast(U32).indirect(listed(pick, first, count))
+                )
+
+            pick_scales(0, 512)
+            pick_words(0, 256)
+
+            h = [keep.tile([P, PACK, S], F32, name="h%d" % g, tag="h%d" % g, align_bytes=64) for g in range(GROUPS)]
+            raw_banks = {}
+            chunks = S // CHUNK
+            mag_c = early.tile([P, chunks, GROUPS * CHUNK], U32, name="mag_c", align_bytes=64)
+            mag_s = early.tile([P, chunks, GROUPS * CHUNK], U8, name="mag_s", align_bytes=64)
+
+            def raw_pass(bank, c, g, t, start):
+                cols = slice(c * CHUNK, (c + 1) * CHUNK)
+                nc.tensor.matmul_mx(
+                    out=bank[:, t * CHUNK : (t + 1) * CHUNK],
+                    lhsT=w1_c[:, g, t * P : (t + 1) * P].bitcast(FP8X4),
+                    lhsT_scale=w1_s[:, g, t * P : (t + 1) * P],
+                    rhs=v_c[:, cols].bitcast(FP8X4),
+                    rhs_scale=v_s[:, cols],
+                    start=start,
+                    stop=True,
+                )
+
+            def first_product(c):
+                mag = early.tile([P, GROUPS, PASS], BF16, name="mag", bufs=2, align_bytes=64)
+                for g in range(GROUPS):
+                    bank = banks[(GROUPS * c + g) % 4]
+                    for t in range(PACK):
+                        raw_pass(bank, c, g, t, True)
+                    nc.scalar.activation(
+                        out=mag[:, g, :].rearrange("p (n t) -> p n t", t=PACK),
+                        in_=bank[:].rearrange("p (t n) -> p n t", t=PACK),
+                        func=ACT.Abs,
+                    )
+                    raw_banks[c, g] = bank
+                nc.vector.quantize_mx(
+                    out=mag_c[:, c, :].bitcast(FP8X4), scales=mag_s[:, c, :], in_=mag[:].rearrange("p g n -> p (g n)")
+                )
+
+            def second_product(c, g):
+                cols = slice(c * CHUNK, (c + 1) * CHUNK)
+                on_vector = g == 0 or c >= REPEATED
+                if on_vector:
+                    raw_sb = early.tile([P, BANK], F32, name="raw_sb", bufs=2)
+                    nc.scalar.copy(out=raw_sb[:], in_=raw_banks[c, g][:])
+                bank = banks[4 + c % 4]
                 for t in range(PACK):
                     for a in range(GROUPS):
                         nc.tensor.matmul_mx(
                             out=bank[:, t * CHUNK : (t + 1) * CHUNK],
-                            lhsT=w2_c[:, t, a, 2 * g * P : 2 * (g + 1) * P].bitcast(FP4X4),
+                            lhsT=w2_c[:, g, t, a, :].bitcast(FP4X4),
                             lhsT_scale=w2_s[:, t, a, g * P : (g + 1) * P],
-                            rhs=mag_c[:, a * CHUNK : (a + 1) * CHUNK].bitcast(FP8X4),
-                            rhs_scale=mag_s[:, a * CHUNK : (a + 1) * CHUNK],
+                            rhs=mag_c[:, c, a * CHUNK : (a + 1) * CHUNK].bitcast(FP8X4),
+                            rhs_scale=mag_s[:, c, a * CHUNK : (a + 1) * CHUNK],
                             start=(a == 0),
                             stop=(on_vector and a == GROUPS - 1),
                         )
@@ -213,44 +214,56 @@ def tile_list_lens_slot_refresh_kernel(
                 sums = bank[:].rearrange("p (t n) -> p t n", t=PACK)
                 if on_vector:
                     nc.vector.tensor_tensor(
-                        out=h[g][:, :, cols],
-                        in0=sums,
-                        in1=raw_sb[:, g, :].rearrange("p (t n) -> p t n", t=PACK),
-                        op=ADD,
+                        out=h[g][:, :, cols], in0=sums, in1=raw_sb[:].rearrange("p (t n) -> p t n", t=PACK), op=ADD
                     )
                 else:
                     nc.scalar.copy(out=h[g][:, :, cols], in_=sums)
 
-        def put_columns(g, t, first, count):
-            nc.vector.tensor_tensor(
-                page[g, t][:].indirect(listed(put, first, count)),
-                h[g][:, t, first : first + count],
-                gate[:, t, first : first + count],
-                MULT,
-            )
+            def put_columns(g, t, first, count):
+                nc.vector.tensor_tensor(
+                    page[g, t][:].indirect(listed(put, first, count)),
+                    h[g][:, t, first : first + count],
+                    gate[:, t, first : first + count],
+                    MULT,
+                )
 
-        chunks = S // CHUNK
-        first_product(0)
-        first_product(1)
-        pick_words(256, 256)
-        pick_scales(512, 512)
-        pick_words(512, 512)
-        for c in range(chunks):
-            second_product(c)
-            if c + 2 < chunks:
-                first_product(c + 2)
-            if c % 2 == 1:
-                for t in range(PACK):
-                    put_columns(0, t, (c // 2) * QUARTER, QUARTER)
+            first_product(0)
+            first_product(1)
+            pick_words(256, 256)
+            pick_scales(512, 512)
+            pick_words(512, 512)
+            for c in range(0, chunks, 2):
+                second_product(c, 0)
+                second_product(c + 1, 0)
+                for t in range(2):
+                    put_columns(0, t, c * CHUNK, QUARTER)
+                if c + 2 < chunks:
+                    first_product(c + 2)
+                    first_product(c + 3)
+            for t in range(2, PACK):
+                put_columns(0, t, 0, S)
+            deal_w2(1)
+            for c in reversed(range(chunks)):
+                second_product(c, 1)
+        late = ctx.enter_context(tc.tile_pool(name="late", bufs=4))
+
+        def rounded_tile():
+            return late.tile([P, PACK * BANK], BF16, name="rounded", bufs=8, align_bytes=64)
+
+        w4_c = keep.tile([P, GROUPS, N], U32, name="w4_c", align_bytes=64)
+        w4_s = keep.tile([P, GROUPS, N], U8, name="w4_s", align_bytes=64)
+        for g in range(GROUPS):
+            quantise_weight(w4_raw[g], nc.scalar.copy, rounded_tile(), w4_c[:, g, :], w4_s[:, g, :])
 
         out_2_words = out_2.rearrange("g p m t -> g p (m t)")
         page_s = [keep.tile([P, T2], U8, name="page_s%d" % g, align_bytes=64) for g in range(GROUPS)]
         pairs = {}
 
         def turn_pair(g, u):
-            pair = stage_tile([P, T2 // P, P, 2], BF16)
+            pair = stage[(1 + 2 * g + u) % 3]
+            rows = pair[:].bitcast(BF16).rearrange("m (b p e) -> m b p e", p=P, e=2)
             for k in range(T2 // (2 * P)):
-                bank = psum.tile([P, BANK], F32, name="left", tag="left")
+                bank = banks[k]
                 for b in range(2):
                     for e in range(2):
                         nc.tensor.transpose(
@@ -259,7 +272,7 @@ def tile_list_lens_slot_refresh_kernel(
                             ident[:],
                         )
                 nc.scalar.copy(
-                    out=pair[:, 2 * k : 2 * k + 2, :, :],
+                    out=rows[:, 2 * k : 2 * k + 2, :, :],
                     in_=bank[:].rearrange("m (b e p) -> m b p e", b=2, e=2),
                 )
             pairs[g, u] = pair
@@ -268,42 +281,49 @@ def tile_list_lens_slot_refresh_kernel(
             for e in range(2):
                 nc.sync.dma_start(out=out_1_rows[g, 2 * u + e], in_=page[g, 2 * u + e][:])
 
-        def page_planes(g):
-            words = [pairs[g, u][:].rearrange("m b p e -> m (b p e)").bitcast(F32) for u in range(2)]
+        def turn_back(g):
+            pieces = []
             for piece in range(T2 // BANK):
                 rounded = rounded_tile()
                 rounded_words = rounded[:].bitcast(F32)
                 for k in range(2):
-                    bank = psum.tile([P, BANK], F32, name="right", tag="right")
+                    bank = banks[2 * piece + k]
                     for b in range(2):
                         block = 4 * piece + 2 * k + b
                         for u in range(2):
                             nc.tensor.transpose(
                                 bank[:, (2 * b + u) * P : (2 * b + u + 1) * P],
-                                words[u][:, block * P : (block + 1) * P],
+                                pairs[g, u][:, block * P : (block + 1) * P],
                                 ident[:],
                             )
                     nc.scalar.copy(
                         out=rounded_words[:, k * BANK : (k + 1) * BANK].rearrange("p (b m u) -> p b m u", b=2, u=2),
                         in_=bank[:].rearrange("p (b u m) -> p b m u", b=2, u=2),
                     )
-                codes = ring.tile([P, BANK], U32, name="page_c", bufs=4, align_bytes=64)
+                pieces.append(rounded)
+            return pieces
+
+        def page_planes(g, pieces, first, codes):
+            for k, rounded in enumerate(pieces):
+                piece = first + k
                 nc.vector.quantize_mx(
-                    out=codes[:].bitcast(FP8X4), scales=page_s[g][:, piece * BANK : (piece + 1) * BANK], in_=rounded[:]
+                    out=codes[:, k * BANK : (k + 1) * BANK].bitcast(FP8X4),
+                    scales=page_s[g][:, piece * BANK : (piece + 1) * BANK],
+                    in_=rounded[:],
                 )
                 nc.sync.dma_start(
                     out=out_2_words[g, :, piece * 4 * BANK : (piece + 1) * 4 * BANK].bitcast(I32),
-                    in_=codes[:].bitcast(I32),
+                    in_=codes[:, k * BANK : (k + 1) * BANK].bitcast(I32),
                 )
-            for q in range(4):
+            cols = slice(first * BANK, (first + len(pieces)) * BANK)
+            for q in (0, 2, 1, 3):
                 nc.sync.dma_start(
-                    out=out_3[g, 4 * q : 4 * q + 4, :].bitcast(I32), in_=page_s[g][32 * q : 32 * q + 4, :].bitcast(I32)
+                    out=out_3[g, 4 * q : 4 * q + 4, cols].bitcast(I32),
+                    in_=page_s[g][32 * q : 32 * q + 4, cols].bitcast(I32),
                 )
 
-        w4_c = keep.tile([P, GROUPS, N], U32, name="w4_c", align_bytes=64)
-        w4_s = keep.tile([P, GROUPS, N], U8, name="w4_s", align_bytes=64)
-        for g in range(GROUPS):
-            quantise_weight(w4_raw[g], nc.scalar.copy, w4_c[:, g, :], w4_s[:, g, :])
+        def codes_tile():
+            return late.tile([P, T2], U32, name="page_c", bufs=1, align_bytes=64)
 
         gm_rows = gm.rearrange("(g p t) j -> g p t j", p=P, t=PACK)
         factor = []
@@ -317,7 +337,7 @@ def tile_list_lens_slot_refresh_kernel(
             turn_pair(0, u)
         for t in range(2):
             put_columns(1, t, 0, S)
-        page_planes(0)
+        page_planes(0, turn_back(0), 0, codes_tile())
         store_pages(1, 0)
         turn_pair(1, 0)
         for t in range(2, PACK):
@@ -325,36 +345,41 @@ def tile_list_lens_slot_refresh_kernel(
         store_pages(1, 1)
         turn_pair(1, 1)
 
-        fetched = keep.tile([P, 2, PACK * BANK], F32, name="fetched", tag="gate", align_bytes=64)
+        fetched = [
+            keep.tile([P, 2, PACK * BANK], F32, name="fetched%d" % k, tag=tag, align_bytes=64)
+            for k, tag in enumerate(("gate", "h1"))
+        ]
         out_0_rows = out_0.rearrange("(p t) j -> p t j", t=PACK)
 
-        def fetch_columns(g, first, count):
-            slot = fetched[:, g, 0 : PACK * count]
+        def fetch_columns(g, i):
+            first, count = X_PIECES[i]
+            slot = fetched[i % 2][:, g, 0 : PACK * count]
             for t in range(PACK):
-                nc.vector.tensor_tensor(
-                    slot[:, t * count : (t + 1) * count],
-                    page[g, t][:].indirect(listed(fetch, first, count)),
-                    factor[g][:, t, first : first + count],
-                    MULT,
-                )
-            rounded = rounded_tile()
+                values = slot[:, t * count : (t + 1) * count]
+                looked_up = page[g, t][:].indirect(listed(fetch, first, count))
+                nc.vector.tensor_tensor(values, looked_up, factor[g][:, t, first : first + count], MULT)
+            if i == 0:
+                rounded = pairs[0, 1][:].bitcast(BF16)[:, g * PACK * count : (g + 1) * PACK * count]
+            else:
+                rounded = late.tile([P, PACK * count], BF16, name="x%d%d" % (g, i), bufs=1, align_bytes=64)[:]
             nc.scalar.copy(
-                out=rounded[:, 0 : PACK * count].rearrange("p (c i t) -> p c t i", i=4, t=PACK),
+                out=rounded.rearrange("p (c i t) -> p c t i", i=4, t=PACK),
                 in_=slot.rearrange("p (t c i) -> p c t i", i=4, t=PACK),
             )
             x_c = ring.tile([P, BANK], U32, name="x_c", bufs=4, align_bytes=64)
             x_s = ring.tile([P, BANK], U8, name="x_s", bufs=4, align_bytes=64)
             nc.vector.quantize_mx(
-                out=x_c[:, 0:count].bitcast(FP8X4), scales=x_s[:, 0:count], in_=rounded[:, 0 : PACK * count]
+                out=x_c[:, 0:count].bitcast(FP8X4), scales=x_s[:, 0:count], in_=rounded
             )
             return x_c, x_s
 
-        def last_product(first, count, xs):
+        def last_product(i, xs):
+            first, count = X_PIECES[i]
             for pair in range(2):
-                y = ring.tile([P, 2, BANK], F32, name="y", tag="f32pair")
+                y = late.tile([P, 2, BANK], F32, name="y")
                 for e in range(2):
                     t = 2 * pair + e
-                    bank = psum.tile([P, BANK], F32, name="left", tag="left")
+                    bank = banks[(PACK * i + t) % 8]
                     for g in range(GROUPS):
                         nc.tensor.matmul_mx(
                             out=bank[:, 0:count],
@@ -372,8 +397,12 @@ def tile_list_lens_slot_refresh_kernel(
                     out=out_0_rows[:, 2 * pair : 2 * pair + 2, first : first + count], in_=y[:, :, 0:count]
                 )
 
-        for i, (first, count) in enumerate(X_PIECES):
-            xs = [fetch_columns(g, first, count) for g in range(GROUPS)]
-            last_product(first, count, xs)
-            if i == 0:
-                page_planes(1)
+        pieces = turn_back(1)
+        xs = {}
+        for i in range(len(X_PIECES) + 1):
+            if i < len(X_PIECES):
+                xs[i] = [fetch_columns(g, i) for g in range(GROUPS)]
+            if i > 0:
+                last_product(i - 1, xs[i - 1])
+        page_planes(1, pieces[0:2], 0, codes_tile())
+        page_planes(1, pieces[2:4], 2, keep.tile([P, T2], U32, name="page_c_last", tag="h0", align_bytes=64))

@@ -54,6 +54,16 @@ def tile_list_lens_slot_refresh_kernel(
             w2_s_raw = early.tile([P, GROUPS, H], U8, name="w2_s_raw", align_bytes=64)
             nc.vector.memset(tab_s[:].bitcast(I32), 0)
             nc.gpsimd.memset(w2_s_raw[:].rearrange("p a c -> p (a c)").bitcast(I32), 0)
+            for q in (0, 2, 1, 3):
+                nc.gpsimd.dma_start(
+                    out=w2_s_raw[32 * q : 32 * q + 4, :, :].bitcast(I32),
+                    in_=w2_scales[:, 4 * q : 4 * q + 4, :].rearrange("a q c -> q a c").bitcast(I32),
+                )
+            for q in (0, 2, 1, 3):
+                nc.gpsimd.dma_start(
+                    out=tab_s[32 * q : 32 * q + 4, :].bitcast(I32),
+                    in_=tab_scales[0, 4 * q : 4 * q + 4, :].bitcast(I32),
+                )
 
             w1_rows = w1.rearrange("(p j) c -> p j c", j=PACK)
             w1_raw = []
@@ -61,17 +71,6 @@ def tile_list_lens_slot_refresh_kernel(
                 raw = stage[g][:].rearrange("p (j c) -> p j c", j=PACK)
                 nc.sync.dma_start(out=raw, in_=w1_rows[:, :, g * PASS : (g + 1) * PASS])
                 w1_raw.append(raw)
-                if g == 0:
-                    for q in (0, 2, 1, 3):
-                        nc.sync.dma_start(
-                            out=tab_s[32 * q : 32 * q + 4, :].bitcast(I32),
-                            in_=tab_scales[0, 4 * q : 4 * q + 4, :].bitcast(I32),
-                        )
-                    for q in (0, 2, 1, 3):
-                        nc.sync.dma_start(
-                            out=w2_s_raw[32 * q : 32 * q + 4, :, :].bitcast(I32),
-                            in_=w2_scales[:, 4 * q : 4 * q + 4, :].rearrange("a q c -> q a c").bitcast(I32),
-                        )
             nc.sync.dma_start(out=pick[:], in_=offs)
             tab_w = keep.tile([P, T], I32, name="tab_w", tag="tab_w", align_bytes=64)
             nc.sync.dma_start(out=tab_w[:], in_=tab_words[0].rearrange("p m t -> p (m t)").bitcast(I32))
@@ -303,27 +302,22 @@ def tile_list_lens_slot_refresh_kernel(
                 pieces.append(rounded)
             return pieces
 
-        def page_planes(g, pieces, first, codes):
-            for k, rounded in enumerate(pieces):
-                piece = first + k
+        def page_words(g, pieces, first, codes):
+            for piece in (first, first + 1):
+                cols = slice(piece * BANK, (piece + 1) * BANK)
                 nc.vector.quantize_mx(
-                    out=codes[:, k * BANK : (k + 1) * BANK].bitcast(FP8X4),
-                    scales=page_s[g][:, piece * BANK : (piece + 1) * BANK],
-                    in_=rounded[:],
+                    out=codes[:, cols].bitcast(FP8X4), scales=page_s[g][:, cols], in_=pieces[piece][:]
                 )
-                nc.sync.dma_start(
-                    out=out_2_words[g, :, piece * 4 * BANK : (piece + 1) * 4 * BANK].bitcast(I32),
-                    in_=codes[:, k * BANK : (k + 1) * BANK].bitcast(I32),
-                )
-            cols = slice(first * BANK, (first + len(pieces)) * BANK)
+            nc.sync.dma_start(
+                out=out_2_words[g, :, first * PACK * BANK : (first + 2) * PACK * BANK].bitcast(I32),
+                in_=codes[:, first * BANK : (first + 2) * BANK].bitcast(I32),
+            )
+
+        def page_scales(g):
             for q in (0, 2, 1, 3):
                 nc.sync.dma_start(
-                    out=out_3[g, 4 * q : 4 * q + 4, cols].bitcast(I32),
-                    in_=page_s[g][32 * q : 32 * q + 4, cols].bitcast(I32),
+                    out=out_3[g, 4 * q : 4 * q + 4, :].bitcast(I32), in_=page_s[g][32 * q : 32 * q + 4, :].bitcast(I32)
                 )
-
-        def codes_tile():
-            return late.tile([P, T2], U32, name="page_c", bufs=1, align_bytes=64)
 
         gm_rows = gm.rearrange("(g p t) j -> g p t j", p=P, t=PACK)
         factor = []
@@ -337,7 +331,11 @@ def tile_list_lens_slot_refresh_kernel(
             turn_pair(0, u)
         for t in range(2):
             put_columns(1, t, 0, S)
-        page_planes(0, turn_back(0), 0, codes_tile())
+        pieces = turn_back(0)
+        first_codes = late.tile([P, T2], U32, name="page_c0", bufs=1, align_bytes=64)
+        for first in (0, 2):
+            page_words(0, pieces, first, first_codes)
+        page_scales(0)
         store_pages(1, 0)
         turn_pair(1, 0)
         for t in range(2, PACK):
@@ -375,27 +373,21 @@ def tile_list_lens_slot_refresh_kernel(
 
         def last_product(i, xs):
             first, count = X_PIECES[i]
-            for pair in range(2):
-                y = late.tile([P, 2, BANK], F32, name="y")
-                for e in range(2):
-                    t = 2 * pair + e
-                    bank = banks[(PACK * i + t) % 8]
-                    for g in range(GROUPS):
-                        nc.tensor.matmul_mx(
-                            out=bank[:, 0:count],
-                            lhsT=w4_c[:, g, t * P : (t + 1) * P].bitcast(FP8X4),
-                            lhsT_scale=w4_s[:, g, t * P : (t + 1) * P],
-                            rhs=xs[g][0][:, 0:count].bitcast(FP8X4),
-                            rhs_scale=xs[g][1][:, 0:count],
-                            start=(g == 0),
-                            stop=(g == GROUPS - 1),
-                        )
-                    nc.scalar.activation(
-                        out=y[:, e, 0:count], in_=bank[:, 0:count], func=ACT.Tanh, bias=bias[:, t : t + 1]
+            y = late.tile([P, PACK, count], F32, name="y%d" % i, bufs=1)
+            for t in range(PACK):
+                bank = banks[(PACK * i + t) % 8]
+                for g in range(GROUPS):
+                    nc.tensor.matmul_mx(
+                        out=bank[:, 0:count],
+                        lhsT=w4_c[:, g, t * P : (t + 1) * P].bitcast(FP8X4),
+                        lhsT_scale=w4_s[:, g, t * P : (t + 1) * P],
+                        rhs=xs[g][0][:, 0:count].bitcast(FP8X4),
+                        rhs_scale=xs[g][1][:, 0:count],
+                        start=(g == 0),
+                        stop=(g == GROUPS - 1),
                     )
-                nc.sync.dma_start(
-                    out=out_0_rows[:, 2 * pair : 2 * pair + 2, first : first + count], in_=y[:, :, 0:count]
-                )
+                nc.scalar.activation(out=y[:, t, :], in_=bank[:, 0:count], func=ACT.Tanh, bias=bias[:, t : t + 1])
+            nc.sync.dma_start(out=out_0_rows[:, :, first : first + count], in_=y[:])
 
         pieces = turn_back(1)
         xs = {}
@@ -404,5 +396,7 @@ def tile_list_lens_slot_refresh_kernel(
                 xs[i] = [fetch_columns(g, i) for g in range(GROUPS)]
             if i > 0:
                 last_product(i - 1, xs[i - 1])
-        page_planes(1, pieces[0:2], 0, codes_tile())
-        page_planes(1, pieces[2:4], 2, keep.tile([P, T2], U32, name="page_c_last", tag="h0", align_bytes=64))
+        last_codes = keep.tile([P, T2], U32, name="page_c1", tag="h0", align_bytes=64)
+        for first in (0, 2):
+            page_words(1, pieces, first, last_codes)
+        page_scales(1)

@@ -54,16 +54,6 @@ def tile_list_lens_slot_refresh_kernel(
             w2_s_raw = early.tile([P, GROUPS, H], U8, name="w2_s_raw", align_bytes=64)
             nc.vector.memset(tab_s[:].bitcast(I32), 0)
             nc.gpsimd.memset(w2_s_raw[:].rearrange("p a c -> p (a c)").bitcast(I32), 0)
-            for q in (0, 2, 1, 3):
-                nc.gpsimd.dma_start(
-                    out=w2_s_raw[32 * q : 32 * q + 4, :, :].bitcast(I32),
-                    in_=w2_scales[:, 4 * q : 4 * q + 4, :].rearrange("a q c -> q a c").bitcast(I32),
-                )
-            for q in (0, 2, 1, 3):
-                nc.gpsimd.dma_start(
-                    out=tab_s[32 * q : 32 * q + 4, :].bitcast(I32),
-                    in_=tab_scales[0, 4 * q : 4 * q + 4, :].bitcast(I32),
-                )
 
             w1_rows = w1.rearrange("(p j) c -> p j c", j=PACK)
             w1_raw = []
@@ -71,11 +61,22 @@ def tile_list_lens_slot_refresh_kernel(
                 raw = stage[g][:].rearrange("p (j c) -> p j c", j=PACK)
                 nc.sync.dma_start(out=raw, in_=w1_rows[:, :, g * PASS : (g + 1) * PASS])
                 w1_raw.append(raw)
+                if g == 0:
+                    for q in (0, 2, 1, 3):
+                        nc.sync.dma_start(
+                            out=tab_s[32 * q : 32 * q + 4, :].bitcast(I32),
+                            in_=tab_scales[0, 4 * q : 4 * q + 4, :].bitcast(I32),
+                        )
             nc.sync.dma_start(out=pick[:], in_=offs)
             tab_w = keep.tile([P, T], I32, name="tab_w", tag="tab_w", align_bytes=64)
             nc.sync.dma_start(out=tab_w[:], in_=tab_words[0].rearrange("p m t -> p (m t)").bitcast(I32))
             w2_raw = early.tile([P, GROUPS, 2 * H], U8, name="w2_raw", align_bytes=64)
             nc.sync.dma_start(out=w2_raw[:].bitcast(I32), in_=w2_words.rearrange("a p c -> p a c").bitcast(I32))
+            for q in (0, 2, 1, 3):
+                nc.sync.dma_start(
+                    out=w2_s_raw[32 * q : 32 * q + 4, :, :].bitcast(I32),
+                    in_=w2_scales[:, 4 * q : 4 * q + 4, :].rearrange("a q c -> q a c").bitcast(I32),
+                )
             nc.sync.dma_start(out=put[:], in_=offs2)
 
             gate = keep.tile([P, PACK, S], F32, name="gate", tag="gate", align_bytes=64)
@@ -129,10 +130,6 @@ def tile_list_lens_slot_refresh_kernel(
 
             w2_c = early.tile([P, GROUPS, PACK, GROUPS, 2 * P], U8, name="w2_c", align_bytes=64)
             w2_s = early.tile([P, PACK, GROUPS, H // PACK], U8, name="w2_s", align_bytes=64)
-            nc.vector.tensor_copy(
-                out=w2_s[:].rearrange("p t a q -> p t (a q)"),
-                in_=w2_s_raw[:].rearrange("p a (q t) -> p t (a q)", t=PACK),
-            )
 
             def deal_w2(g):
                 nc.scalar.copy(
@@ -155,6 +152,11 @@ def tile_list_lens_slot_refresh_kernel(
 
             pick_scales(0, 512)
             pick_words(0, 256)
+            nc.vector.tensor_copy(
+                out=w2_s[:].rearrange("p t a q -> p t (a q)"),
+                in_=w2_s_raw[:].rearrange("p a (q t) -> p t (a q)", t=PACK),
+            )
+
 
             h = [keep.tile([P, PACK, S], F32, name="h%d" % g, tag="h%d" % g, align_bytes=64) for g in range(GROUPS)]
             raw_banks = {}
@@ -177,7 +179,7 @@ def tile_list_lens_slot_refresh_kernel(
             def first_product(c):
                 mag = early.tile([P, GROUPS, PASS], BF16, name="mag", bufs=2, align_bytes=64)
                 for g in range(GROUPS):
-                    bank = banks[(GROUPS * c + g) % 4]
+                    bank = banks[c % 4] if g == 0 else banks[4 + c % 2]
                     for t in range(PACK):
                         raw_pass(bank, c, g, t, True)
                     nc.scalar.activation(
@@ -196,7 +198,7 @@ def tile_list_lens_slot_refresh_kernel(
                 if on_vector:
                     raw_sb = early.tile([P, BANK], F32, name="raw_sb", bufs=2)
                     nc.scalar.copy(out=raw_sb[:], in_=raw_banks[c, g][:])
-                bank = banks[4 + c % 4]
+                bank = banks[6 + c % 2] if g == 0 else banks[c % 4]
                 for t in range(PACK):
                     for a in range(GROUPS):
                         nc.tensor.matmul_mx(
@@ -229,6 +231,8 @@ def tile_list_lens_slot_refresh_kernel(
             first_product(0)
             first_product(1)
             pick_words(256, 256)
+            first_product(2)
+            first_product(3)
             pick_scales(512, 512)
             pick_words(512, 512)
             for c in range(0, chunks, 2):
@@ -236,9 +240,9 @@ def tile_list_lens_slot_refresh_kernel(
                 second_product(c + 1, 0)
                 for t in range(2):
                     put_columns(0, t, c * CHUNK, QUARTER)
-                if c + 2 < chunks:
-                    first_product(c + 2)
-                    first_product(c + 3)
+                if c + 4 < chunks:
+                    first_product(c + 4)
+                    first_product(c + 5)
             for t in range(2, PACK):
                 put_columns(0, t, 0, S)
             deal_w2(1)
@@ -303,14 +307,16 @@ def tile_list_lens_slot_refresh_kernel(
             return pieces
 
         def page_words(g, pieces, first, codes):
-            for piece in (first, first + 1):
-                cols = slice(piece * BANK, (piece + 1) * BANK)
+            for k in range(2):
+                piece = first + k
                 nc.vector.quantize_mx(
-                    out=codes[:, cols].bitcast(FP8X4), scales=page_s[g][:, cols], in_=pieces[piece][:]
+                    out=codes[:, k * BANK : (k + 1) * BANK].bitcast(FP8X4),
+                    scales=page_s[g][:, piece * BANK : (piece + 1) * BANK],
+                    in_=pieces[piece][:],
                 )
             nc.sync.dma_start(
                 out=out_2_words[g, :, first * PACK * BANK : (first + 2) * PACK * BANK].bitcast(I32),
-                in_=codes[:, first * BANK : (first + 2) * BANK].bitcast(I32),
+                in_=codes[:].bitcast(I32),
             )
 
         def page_scales(g):
@@ -332,9 +338,8 @@ def tile_list_lens_slot_refresh_kernel(
         for t in range(2):
             put_columns(1, t, 0, S)
         pieces = turn_back(0)
-        first_codes = late.tile([P, T2], U32, name="page_c0", bufs=1, align_bytes=64)
         for first in (0, 2):
-            page_words(0, pieces, first, first_codes)
+            page_words(0, pieces, first, late.tile([P, 2 * BANK], U32, name="page_c0", bufs=2, align_bytes=64))
         page_scales(0)
         store_pages(1, 0)
         turn_pair(1, 0)
@@ -359,7 +364,7 @@ def tile_list_lens_slot_refresh_kernel(
             if i == 0:
                 rounded = pairs[0, 1][:].bitcast(BF16)[:, g * PACK * count : (g + 1) * PACK * count]
             else:
-                rounded = late.tile([P, PACK * count], BF16, name="x%d%d" % (g, i), bufs=1, align_bytes=64)[:]
+                rounded = late.tile([P, PACK * count], BF16, name="x%d%d" % (g, i), tag="x%d%d" % (g, i), bufs=1, align_bytes=64)[:]
             nc.scalar.copy(
                 out=rounded.rearrange("p (c i t) -> p c t i", i=4, t=PACK),
                 in_=slot.rearrange("p (t c i) -> p c t i", i=4, t=PACK),
@@ -396,7 +401,6 @@ def tile_list_lens_slot_refresh_kernel(
                 xs[i] = [fetch_columns(g, i) for g in range(GROUPS)]
             if i > 0:
                 last_product(i - 1, xs[i - 1])
-        last_codes = keep.tile([P, T2], U32, name="page_c1", tag="h0", align_bytes=64)
-        for first in (0, 2):
-            page_words(1, pieces, first, last_codes)
+        page_words(1, pieces, 0, keep.tile([P, 2 * BANK], U32, name="page_c10", tag="h0", align_bytes=64))
+        page_words(1, pieces, 2, late.tile([P, 2 * BANK], U32, name="page_c11", tag="x13", bufs=1, align_bytes=64))
         page_scales(1)

@@ -23,9 +23,12 @@ PACK = 4
 PASS = P * PACK
 GROUPS = H // PASS
 BANK = 512
-CHUNK = 128
-QUARTER = 256
-REPEATED = 6
+CHUNK = BANK // PACK
+CHUNKS = S // CHUNK
+QUARTER = 2 * CHUNK
+QUADRANTS = (0, 2, 1, 3)
+ADDED_ON_VECTOR = 4
+REPEATED = 2
 X_PIECES = ((0, 512), (512, 256), (768, 128), (896, 128))
 
 
@@ -39,12 +42,13 @@ def tile_list_lens_slot_refresh_kernel(
         keep = ctx.enter_context(tc.tile_pool(name="keep", bufs=1))
         ring = ctx.enter_context(tc.tile_pool(name="ring", bufs=2))
         psum = ctx.enter_context(tc.psum_pool(name="psum", bufs=1))
-        banks = [psum.tile([P, BANK], F32, name="bank%d" % k) for k in range(8)]
-        stage = [keep.tile([P, PACK * PASS], F32, name="stage%d" % k, align_bytes=64) for k in range(3)]
+        banks = [psum.tile([P, BANK], F32, name="bank%d" % b) for b in range(8)]
+        stage = [keep.tile([P, PACK * PASS], F32, name="stage%d" % b, align_bytes=64) for b in range(3)]
+
         with tc.tile_pool(name="early", bufs=1) as early:
 
-            def listed(tile, first, count):
-                return tile[:, first // 16 : (first + count) // 16]
+            def listed(offsets, first, count):
+                return offsets[:, first // 16 : (first + count) // 16]
 
             pick = lists.tile([P, S // 16], U16, name="pick")
             put = lists.tile([P, S // 16], U16, name="put")
@@ -56,26 +60,26 @@ def tile_list_lens_slot_refresh_kernel(
             nc.gpsimd.memset(w2_s_raw[:].rearrange("p a c -> p (a c)").bitcast(I32), 0)
 
             w1_rows = w1.rearrange("(p j) c -> p j c", j=PACK)
-            w1_raw = []
+            w1_loaded = []
             for g in range(GROUPS):
-                raw = stage[g][:].rearrange("p (j c) -> p j c", j=PACK)
-                nc.sync.dma_start(out=raw, in_=w1_rows[:, :, g * PASS : (g + 1) * PASS])
-                w1_raw.append(raw)
+                loaded = stage[g][:].rearrange("p (j c) -> p j c", j=PACK)
+                nc.sync.dma_start(out=loaded, in_=w1_rows[:, :, g * PASS : (g + 1) * PASS])
+                w1_loaded.append(loaded)
                 if g == 0:
-                    for q in (0, 2, 1, 3):
+                    for quad in QUADRANTS:
                         nc.sync.dma_start(
-                            out=tab_s[32 * q : 32 * q + 4, :].bitcast(I32),
-                            in_=tab_scales[0, 4 * q : 4 * q + 4, :].bitcast(I32),
+                            out=tab_s[32 * quad : 32 * quad + 4, :].bitcast(I32),
+                            in_=tab_scales[0, 4 * quad : 4 * quad + 4, :].bitcast(I32),
                         )
             nc.sync.dma_start(out=pick[:], in_=offs)
             tab_w = keep.tile([P, T], I32, name="tab_w", tag="tab_w", align_bytes=64)
             nc.sync.dma_start(out=tab_w[:], in_=tab_words[0].rearrange("p m t -> p (m t)").bitcast(I32))
             w2_raw = early.tile([P, GROUPS, 2 * H], U8, name="w2_raw", align_bytes=64)
             nc.sync.dma_start(out=w2_raw[:].bitcast(I32), in_=w2_words.rearrange("a p c -> p a c").bitcast(I32))
-            for q in (0, 2, 1, 3):
+            for quad in QUADRANTS:
                 nc.sync.dma_start(
-                    out=w2_s_raw[32 * q : 32 * q + 4, :, :].bitcast(I32),
-                    in_=w2_scales[:, 4 * q : 4 * q + 4, :].rearrange("a q c -> q a c").bitcast(I32),
+                    out=w2_s_raw[32 * quad : 32 * quad + 4, :, :].bitcast(I32),
+                    in_=w2_scales[:, 4 * quad : 4 * quad + 4, :].rearrange("a q c -> q a c").bitcast(I32),
                 )
             nc.sync.dma_start(out=put[:], in_=offs2)
 
@@ -84,8 +88,8 @@ def tile_list_lens_slot_refresh_kernel(
 
             def load_gate(u, first, count):
                 rows, cols = slice(2 * u, 2 * u + 2), slice(first, first + count)
-                for q in (0, 2, 1, 3):
-                    nc.sync.dma_start(out=gate[32 * q : 32 * q + 32, rows, cols], in_=wgs_rows[:, rows, cols])
+                for quad in QUADRANTS:
+                    nc.sync.dma_start(out=gate[32 * quad : 32 * quad + 32, rows, cols], in_=wgs_rows[:, rows, cols])
 
             page0_rows = page0.rearrange("(g p t) m -> g t p m", p=P, t=PACK)
             out_1_rows = out_1.rearrange("(g p t) m -> g t p m", p=P, t=PACK)
@@ -106,24 +110,28 @@ def tile_list_lens_slot_refresh_kernel(
             ident = keep.tile([P, P], F32, name="ident")
             make_identity(nc, ident[:])
 
-            def quantise_weight(raw, copy, rounded, codes, scales):
+            def quantise_weight(loaded, copy, rounded, codes, scales):
                 copy(
                     out=rounded[:].rearrange("p (t m j) -> p m j t", t=PACK, j=PACK),
-                    in_=raw.rearrange("p j (m t) -> p m j t", t=PACK),
+                    in_=loaded.rearrange("p j (m t) -> p m j t", t=PACK),
                 )
                 nc.vector.quantize_mx(out=codes.bitcast(FP8X4), scales=scales, in_=rounded[:])
 
             w1_c = early.tile([P, GROUPS, PASS], U32, name="w1_c", align_bytes=64)
             w1_s = early.tile([P, GROUPS, PASS], U8, name="w1_s", align_bytes=64)
             for g, copy in enumerate((nc.vector.tensor_copy, nc.scalar.copy)):
-                rounded = early.tile([P, PACK * PASS], BF16, name="w1_rounded", bufs=2, align_bytes=64)
-                quantise_weight(w1_raw[g], copy, rounded, w1_c[:, g, :], w1_s[:, g, :])
+                w1_rounded = early.tile(
+                    [P, PACK * PASS], BF16, name="w1_rounded", tag="w1_rounded", bufs=2, align_bytes=64
+                )
+                quantise_weight(w1_loaded[g], copy, w1_rounded, w1_c[:, g, :], w1_s[:, g, :])
 
-            w4_raw = []
+            w4_loaded = []
             for g in range(GROUPS):
-                raw = stage[(2 + g) % 3][:].rearrange("p (j c) -> p j c", j=PACK)
-                nc.sync.dma_start(out=raw, in_=w4[g * PASS : (g + 1) * PASS, :].rearrange("(p j) c -> p j c", j=PACK))
-                w4_raw.append(raw)
+                loaded = stage[(2 + g) % 3][:].rearrange("p (j c) -> p j c", j=PACK)
+                nc.sync.dma_start(
+                    out=loaded, in_=w4[g * PASS : (g + 1) * PASS, :].rearrange("(p j) c -> p j c", j=PACK)
+                )
+                w4_loaded.append(loaded)
             nc.sync.dma_start(out=fetch[:], in_=offs3)
             bias = keep.tile([P, PACK], F32, name="bias")
             nc.sync.dma_start(out=bias[:], in_=b4.rearrange("(p t) -> p t", t=PACK))
@@ -150,19 +158,17 @@ def tile_list_lens_slot_refresh_kernel(
                     v_c[:, first : first + count], tab_w[:].bitcast(U32).indirect(listed(pick, first, count))
                 )
 
-            pick_scales(0, 512)
-            pick_words(0, 256)
+            pick_scales(0, S // 2)
+            pick_words(0, QUARTER)
             nc.vector.tensor_copy(
                 out=w2_s[:].rearrange("p t a q -> p t (a q)"),
                 in_=w2_s_raw[:].rearrange("p a (q t) -> p t (a q)", t=PACK),
             )
 
-
             h = [keep.tile([P, PACK, S], F32, name="h%d" % g, tag="h%d" % g, align_bytes=64) for g in range(GROUPS)]
             raw_banks = {}
-            chunks = S // CHUNK
-            mag_c = early.tile([P, chunks, GROUPS * CHUNK], U32, name="mag_c", align_bytes=64)
-            mag_s = early.tile([P, chunks, GROUPS * CHUNK], U8, name="mag_s", align_bytes=64)
+            mag_c = early.tile([P, CHUNKS, GROUPS * CHUNK], U32, name="mag_c", align_bytes=64)
+            mag_s = early.tile([P, CHUNKS, GROUPS * CHUNK], U8, name="mag_s", align_bytes=64)
 
             def raw_pass(bank, c, g, t, start):
                 cols = slice(c * CHUNK, (c + 1) * CHUNK)
@@ -192,33 +198,57 @@ def tile_list_lens_slot_refresh_kernel(
                     out=mag_c[:, c, :].bitcast(FP8X4), scales=mag_s[:, c, :], in_=mag[:].rearrange("p g n -> p (g n)")
                 )
 
-            def second_product(c, g):
-                cols = slice(c * CHUNK, (c + 1) * CHUNK)
-                on_vector = g == 0 or c >= REPEATED
-                if on_vector:
-                    raw_sb = early.tile([P, BANK], F32, name="raw_sb", bufs=2)
-                    nc.scalar.copy(out=raw_sb[:], in_=raw_banks[c, g][:])
-                bank = banks[6 + c % 2] if g == 0 else banks[c % 4]
-                for t in range(PACK):
-                    for a in range(GROUPS):
-                        nc.tensor.matmul_mx(
-                            out=bank[:, t * CHUNK : (t + 1) * CHUNK],
-                            lhsT=w2_c[:, g, t, a, :].bitcast(FP4X4),
-                            lhsT_scale=w2_s[:, t, a, g * P : (g + 1) * P],
-                            rhs=mag_c[:, c, a * CHUNK : (a + 1) * CHUNK].bitcast(FP8X4),
-                            rhs_scale=mag_s[:, c, a * CHUNK : (a + 1) * CHUNK],
-                            start=(a == 0),
-                            stop=(on_vector and a == GROUPS - 1),
-                        )
-                    if not on_vector:
-                        raw_pass(bank, c, g, t, False)
-                sums = bank[:].rearrange("p (t n) -> p t n", t=PACK)
-                if on_vector:
-                    nc.vector.tensor_tensor(
-                        out=h[g][:, :, cols], in0=sums, in1=raw_sb[:].rearrange("p (t n) -> p t n", t=PACK), op=ADD
+            def mix_passes(bank, c, g, t, stop):
+                for a in range(GROUPS):
+                    nc.tensor.matmul_mx(
+                        out=bank[:, t * CHUNK : (t + 1) * CHUNK],
+                        lhsT=w2_c[:, g, t, a, :].bitcast(FP4X4),
+                        lhsT_scale=w2_s[:, t, a, g * P : (g + 1) * P],
+                        rhs=mag_c[:, c, a * CHUNK : (a + 1) * CHUNK].bitcast(FP8X4),
+                        rhs_scale=mag_s[:, c, a * CHUNK : (a + 1) * CHUNK],
+                        start=(a == 0),
+                        stop=(stop and a == GROUPS - 1),
                     )
-                else:
-                    nc.scalar.copy(out=h[g][:, :, cols], in_=sums)
+
+            def by_slice(columns):
+                return columns.rearrange("p (t n) -> p t n", t=PACK)
+
+            def h_chunk(c, g):
+                return h[g][:, :, c * CHUNK : (c + 1) * CHUNK]
+
+            def keep_raw(c, g, bufs):
+                raw_sb = early.tile([P, BANK], F32, name="raw_sb%d" % g, bufs=bufs)
+                nc.scalar.copy(out=raw_sb[:], in_=raw_banks[c, g][:])
+                return raw_sb
+
+            def add_on_vector(c, g, bank):
+                raw_sb = keep_raw(c, g, 2)
+                for t in range(PACK):
+                    mix_passes(bank, c, g, t, True)
+                nc.vector.tensor_tensor(out=h_chunk(c, g), in0=by_slice(bank[:]), in1=by_slice(raw_sb[:]), op=ADD)
+
+            def add_by_repeat(c, g, bank):
+                for t in range(PACK):
+                    mix_passes(bank, c, g, t, False)
+                    raw_pass(bank, c, g, t, False)
+                nc.scalar.copy(out=h_chunk(c, g), in_=by_slice(bank[:]))
+
+            def add_by_transposes(c, g, raw_sb, mixed, turned, back):
+                staged = early.tile([P, 2, BANK], F32, name="staged", tag="w1_rounded", bufs=2, align_bytes=64)
+                for t in range(PACK):
+                    mix_passes(mixed, c, g, t, True)
+                nc.scalar.copy(out=staged[:, 0, :], in_=mixed[:])
+                for t in range(PACK):
+                    cols = slice(t * P, (t + 1) * P)
+                    for opens, term in ((True, staged[:, 0, cols]), (False, raw_sb[:, cols])):
+                        nc.tensor.matmul(
+                            turned[:, cols], lhsT=term, rhs=ident[:], is_transpose=True, start=opens, stop=not opens
+                        )
+                nc.scalar.copy(out=staged[:, 1, :], in_=turned[:])
+                for t in range(PACK):
+                    cols = slice(t * P, (t + 1) * P)
+                    nc.tensor.transpose(back[:, cols], staged[:, 1, cols], ident[:])
+                nc.scalar.copy(out=h_chunk(c, g), in_=by_slice(back[:]))
 
             def put_columns(g, t, first, count):
                 nc.vector.tensor_tensor(
@@ -230,24 +260,33 @@ def tile_list_lens_slot_refresh_kernel(
 
             first_product(0)
             first_product(1)
-            pick_words(256, 256)
+            pick_words(QUARTER, QUARTER)
             first_product(2)
             first_product(3)
-            pick_scales(512, 512)
-            pick_words(512, 512)
-            for c in range(0, chunks, 2):
-                second_product(c, 0)
-                second_product(c + 1, 0)
+            pick_scales(S // 2, S // 2)
+            pick_words(S // 2, S // 2)
+            raw_kept = {}
+            for c in range(0, CHUNKS, 2):
+                for chunk in (c, c + 1):
+                    if chunk < ADDED_ON_VECTOR:
+                        add_on_vector(chunk, 0, banks[6 + chunk % 2])
+                    else:
+                        add_by_repeat(chunk, 0, banks[6 + chunk % 2])
                 for t in range(2):
                     put_columns(0, t, c * CHUNK, QUARTER)
-                if c + 4 < chunks:
+                for chunk in (c + 2, c + 3):
+                    if REPEATED <= chunk < CHUNKS:
+                        raw_kept[chunk] = keep_raw(chunk, 1, CHUNKS - REPEATED)
+                if c + 4 < CHUNKS:
                     first_product(c + 4)
                     first_product(c + 5)
             for t in range(2, PACK):
                 put_columns(0, t, 0, S)
             deal_w2(1)
-            for c in reversed(range(chunks)):
-                second_product(c, 1)
+            for c in range(REPEATED, CHUNKS):
+                add_by_transposes(c, 1, raw_kept[c], banks[c % 2], banks[2 + c % 2], banks[4 + c % 2])
+            for c in range(REPEATED):
+                add_by_repeat(c, 1, banks[6 + c % 2])
         late = ctx.enter_context(tc.tile_pool(name="late", bufs=4))
 
         def rounded_tile():
@@ -256,7 +295,7 @@ def tile_list_lens_slot_refresh_kernel(
         w4_c = keep.tile([P, GROUPS, N], U32, name="w4_c", align_bytes=64)
         w4_s = keep.tile([P, GROUPS, N], U8, name="w4_s", align_bytes=64)
         for g in range(GROUPS):
-            quantise_weight(w4_raw[g], nc.scalar.copy, rounded_tile(), w4_c[:, g, :], w4_s[:, g, :])
+            quantise_weight(w4_loaded[g], nc.scalar.copy, rounded_tile(), w4_c[:, g, :], w4_s[:, g, :])
 
         out_2_words = out_2.rearrange("g p m t -> g p (m t)")
         page_s = [keep.tile([P, T2], U8, name="page_s%d" % g, align_bytes=64) for g in range(GROUPS)]
@@ -264,18 +303,19 @@ def tile_list_lens_slot_refresh_kernel(
 
         def turn_pair(g, u):
             pair = stage[(1 + 2 * g + u) % 3]
-            rows = pair[:].bitcast(BF16).rearrange("m (b p e) -> m b p e", p=P, e=2)
-            for k in range(T2 // (2 * P)):
-                bank = banks[k]
+            halves = pair[:].bitcast(BF16).rearrange("m (b p e) -> m b p e", p=P, e=2)
+            for two_blocks in range(T2 // (2 * P)):
+                bank = banks[two_blocks]
                 for b in range(2):
+                    block = 2 * two_blocks + b
                     for e in range(2):
                         nc.tensor.transpose(
                             bank[:, (2 * b + e) * P : (2 * b + e + 1) * P],
-                            page[g, 2 * u + e][:, (2 * k + b) * P : (2 * k + b + 1) * P],
+                            page[g, 2 * u + e][:, block * P : (block + 1) * P],
                             ident[:],
                         )
                 nc.scalar.copy(
-                    out=rows[:, 2 * k : 2 * k + 2, :, :],
+                    out=halves[:, 2 * two_blocks : 2 * two_blocks + 2, :, :],
                     in_=bank[:].rearrange("m (b e p) -> m b p e", b=2, e=2),
                 )
             pairs[g, u] = pair
@@ -285,14 +325,14 @@ def tile_list_lens_slot_refresh_kernel(
                 nc.sync.dma_start(out=out_1_rows[g, 2 * u + e], in_=page[g, 2 * u + e][:])
 
         def turn_back(g):
-            pieces = []
+            rounded_pieces = []
             for piece in range(T2 // BANK):
                 rounded = rounded_tile()
                 rounded_words = rounded[:].bitcast(F32)
-                for k in range(2):
-                    bank = banks[2 * piece + k]
+                for half in range(2):
+                    bank = banks[2 * piece + half]
                     for b in range(2):
-                        block = 4 * piece + 2 * k + b
+                        block = 4 * piece + 2 * half + b
                         for u in range(2):
                             nc.tensor.transpose(
                                 bank[:, (2 * b + u) * P : (2 * b + u + 1) * P],
@@ -300,46 +340,49 @@ def tile_list_lens_slot_refresh_kernel(
                                 ident[:],
                             )
                     nc.scalar.copy(
-                        out=rounded_words[:, k * BANK : (k + 1) * BANK].rearrange("p (b m u) -> p b m u", b=2, u=2),
+                        out=rounded_words[:, half * BANK : (half + 1) * BANK].rearrange(
+                            "p (b m u) -> p b m u", b=2, u=2
+                        ),
                         in_=bank[:].rearrange("p (b u m) -> p b m u", b=2, u=2),
                     )
-                pieces.append(rounded)
-            return pieces
+                rounded_pieces.append(rounded)
+            return rounded_pieces
 
-        def page_words(g, pieces, first, codes):
-            for k in range(2):
-                piece = first + k
+        def page_words(g, rounded_pieces, first_piece, codes):
+            for half in range(2):
+                piece = first_piece + half
                 nc.vector.quantize_mx(
-                    out=codes[:, k * BANK : (k + 1) * BANK].bitcast(FP8X4),
+                    out=codes[:, half * BANK : (half + 1) * BANK].bitcast(FP8X4),
                     scales=page_s[g][:, piece * BANK : (piece + 1) * BANK],
-                    in_=pieces[piece][:],
+                    in_=rounded_pieces[piece][:],
                 )
             nc.sync.dma_start(
-                out=out_2_words[g, :, first * PACK * BANK : (first + 2) * PACK * BANK].bitcast(I32),
+                out=out_2_words[g, :, first_piece * PACK * BANK : (first_piece + 2) * PACK * BANK].bitcast(I32),
                 in_=codes[:].bitcast(I32),
             )
 
         def page_scales(g):
-            for q in (0, 2, 1, 3):
+            for quad in QUADRANTS:
                 nc.sync.dma_start(
-                    out=out_3[g, 4 * q : 4 * q + 4, :].bitcast(I32), in_=page_s[g][32 * q : 32 * q + 4, :].bitcast(I32)
+                    out=out_3[g, 4 * quad : 4 * quad + 4, :].bitcast(I32),
+                    in_=page_s[g][32 * quad : 32 * quad + 4, :].bitcast(I32),
                 )
 
         gm_rows = gm.rearrange("(g p t) j -> g p t j", p=P, t=PACK)
         factor = []
         for g, tag in enumerate(("tab_w", "h0")):
-            tile = keep.tile([P, PACK, PICKS], F32, name="factor%d" % g, tag=tag, align_bytes=64)
-            nc.sync.dma_start(out=tile[:], in_=gm_rows[g])
-            factor.append(tile)
+            factor.append(keep.tile([P, PACK, PICKS], F32, name="factor%d" % g, tag=tag, align_bytes=64))
+            nc.sync.dma_start(out=factor[g][:], in_=gm_rows[g])
 
         for u in range(2):
             store_pages(0, u)
             turn_pair(0, u)
         for t in range(2):
             put_columns(1, t, 0, S)
-        pieces = turn_back(0)
-        for first in (0, 2):
-            page_words(0, pieces, first, late.tile([P, 2 * BANK], U32, name="page_c0", bufs=2, align_bytes=64))
+        group_0_pieces = turn_back(0)
+        for first_piece in (0, 2):
+            codes_0 = late.tile([P, 2 * BANK], U32, name="page_c0", bufs=2, align_bytes=64)
+            page_words(0, group_0_pieces, first_piece, codes_0)
         page_scales(0)
         store_pages(1, 0)
         turn_pair(1, 0)
@@ -349,58 +392,62 @@ def tile_list_lens_slot_refresh_kernel(
         turn_pair(1, 1)
 
         fetched = [
-            keep.tile([P, 2, PACK * BANK], F32, name="fetched%d" % k, tag=tag, align_bytes=64)
-            for k, tag in enumerate(("gate", "h1"))
+            keep.tile([P, GROUPS, PACK * BANK], F32, name="fetched%d" % b, tag=tag, align_bytes=64)
+            for b, tag in enumerate(("gate", "h1"))
         ]
         out_0_rows = out_0.rearrange("(p t) j -> p t j", t=PACK)
 
         def fetch_columns(g, i):
             first, count = X_PIECES[i]
-            slot = fetched[i % 2][:, g, 0 : PACK * count]
+            values = fetched[i % 2][:, g, 0 : PACK * count]
             for t in range(PACK):
-                values = slot[:, t * count : (t + 1) * count]
                 looked_up = page[g, t][:].indirect(listed(fetch, first, count))
-                nc.vector.tensor_tensor(values, looked_up, factor[g][:, t, first : first + count], MULT)
+                nc.vector.tensor_tensor(
+                    values[:, t * count : (t + 1) * count], looked_up, factor[g][:, t, first : first + count], MULT
+                )
             if i == 0:
-                rounded = pairs[0, 1][:].bitcast(BF16)[:, g * PACK * count : (g + 1) * PACK * count]
+                x_rounded = pairs[0, 1][:].bitcast(BF16)[:, g * PACK * count : (g + 1) * PACK * count]
             else:
-                rounded = late.tile([P, PACK * count], BF16, name="x%d%d" % (g, i), tag="x%d%d" % (g, i), bufs=1, align_bytes=64)[:]
+                label = "x%d%d" % (g, i)
+                x_rounded = late.tile([P, PACK * count], BF16, name=label, tag=label, bufs=1, align_bytes=64)[:]
             nc.scalar.copy(
-                out=rounded.rearrange("p (c i t) -> p c t i", i=4, t=PACK),
-                in_=slot.rearrange("p (t c i) -> p c t i", i=4, t=PACK),
+                out=x_rounded.rearrange("p (c n t) -> p c t n", n=4, t=PACK),
+                in_=values.rearrange("p (t c n) -> p c t n", n=4, t=PACK),
             )
             x_c = ring.tile([P, BANK], U32, name="x_c", bufs=4, align_bytes=64)
             x_s = ring.tile([P, BANK], U8, name="x_s", bufs=4, align_bytes=64)
-            nc.vector.quantize_mx(
-                out=x_c[:, 0:count].bitcast(FP8X4), scales=x_s[:, 0:count], in_=rounded
-            )
+            nc.vector.quantize_mx(out=x_c[:, 0:count].bitcast(FP8X4), scales=x_s[:, 0:count], in_=x_rounded)
             return x_c, x_s
 
-        def last_product(i, xs):
+        def last_product(i, x_planes):
             first, count = X_PIECES[i]
             y = late.tile([P, PACK, count], F32, name="y%d" % i, bufs=1)
             for t in range(PACK):
-                bank = banks[(PACK * i + t) % 8]
+                bank = banks[(PACK * i + t) % len(banks)]
                 for g in range(GROUPS):
+                    x_c, x_s = x_planes[g]
                     nc.tensor.matmul_mx(
                         out=bank[:, 0:count],
                         lhsT=w4_c[:, g, t * P : (t + 1) * P].bitcast(FP8X4),
                         lhsT_scale=w4_s[:, g, t * P : (t + 1) * P],
-                        rhs=xs[g][0][:, 0:count].bitcast(FP8X4),
-                        rhs_scale=xs[g][1][:, 0:count],
+                        rhs=x_c[:, 0:count].bitcast(FP8X4),
+                        rhs_scale=x_s[:, 0:count],
                         start=(g == 0),
                         stop=(g == GROUPS - 1),
                     )
                 nc.scalar.activation(out=y[:, t, :], in_=bank[:, 0:count], func=ACT.Tanh, bias=bias[:, t : t + 1])
             nc.sync.dma_start(out=out_0_rows[:, :, first : first + count], in_=y[:])
 
-        pieces = turn_back(1)
-        xs = {}
+        group_1_pieces = turn_back(1)
+        x_pieces = {}
         for i in range(len(X_PIECES) + 1):
             if i < len(X_PIECES):
-                xs[i] = [fetch_columns(g, i) for g in range(GROUPS)]
+                x_pieces[i] = [fetch_columns(g, i) for g in range(GROUPS)]
             if i > 0:
-                last_product(i - 1, xs[i - 1])
-        page_words(1, pieces, 0, keep.tile([P, 2 * BANK], U32, name="page_c10", tag="h0", align_bytes=64))
-        page_words(1, pieces, 2, late.tile([P, 2 * BANK], U32, name="page_c11", tag="x13", bufs=1, align_bytes=64))
+                last_product(i - 1, x_pieces[i - 1])
+        last_x = "x%d%d" % (GROUPS - 1, len(X_PIECES) - 1)
+        codes_10 = keep.tile([P, 2 * BANK], U32, name="page_c10", tag="h0", align_bytes=64)
+        page_words(1, group_1_pieces, 0, codes_10)
+        codes_11 = late.tile([P, 2 * BANK], U32, name="page_c11", tag=last_x, bufs=1, align_bytes=64)
+        page_words(1, group_1_pieces, 2, codes_11)
         page_scales(1)

from contextlib import ExitStack

import concourse.mybir as mybir
from concourse.masks import make_identity

K, T, S, H, T2, PICKS, N = 512, 4096, 1024, 1024, 2048, 1024, 512
FLOPS = 2 * (K * H * S + H * H * S + H * N * PICKS)

F32 = mybir.dt.float32
BF16 = mybir.dt.bfloat16
I32 = mybir.dt.int32
U32 = mybir.dt.uint32
U16 = mybir.dt.uint16
U8 = mybir.dt.uint8
FP8X4 = mybir.dt.float8_e4m3fn_x4
FP4X4 = mybir.dt.float4_e2m1fn_x4
ACT = mybir.ActivationFunctionType
MULT = mybir.AluOpType.mult
ADD = mybir.AluOpType.add

P = 128
PACK = 4
PASS = P * PACK
GROUPS = H // PASS
BANK = 512
CHUNK = BANK // PACK
CHUNKS = S // CHUNK
QUARTER = 2 * CHUNK
QUADRANTS = (0, 2, 1, 3)
ADDED_ON_VECTOR = 4
REPEATED = 2
X_PIECES = ((0, 512), (512, 256), (768, 128), (896, 128))


def tile_list_lens_slot_refresh_kernel(
    tc, tab_words, tab_scales, offs, offs2, offs3, w1, w2_words, w2_scales, wgs, page0, gm, w4, b4,
    out_0, out_1, out_2, out_3,
):
    nc = tc.nc
    with ExitStack() as ctx:
        lists = ctx.enter_context(tc.tile_pool(name="lists", bufs=1))
        keep = ctx.enter_context(tc.tile_pool(name="keep", bufs=1))
        ring = ctx.enter_context(tc.tile_pool(name="ring", bufs=2))
        psum = ctx.enter_context(tc.psum_pool(name="psum", bufs=1))
        banks = [psum.tile([P, BANK], F32, name="bank%d" % b) for b in range(8)]
        stage = [keep.tile([P, PACK * PASS], F32, name="stage%d" % b, align_bytes=64) for b in range(3)]

        with tc.tile_pool(name="early", bufs=1) as early:

            def listed(offsets, first, count):
                return offsets[:, first // 16 : (first + count) // 16]

            pick = lists.tile([P, S // 16], U16, name="pick")
            put = lists.tile([P, S // 16], U16, name="put")
            fetch = lists.tile([P, PICKS // 16], U16, name="fetch")

            tab_s = early.tile([P, T], U8, name="tab_s", align_bytes=64)
            w2_s_raw = early.tile([P, GROUPS, H], U8, name="w2_s_raw", align_bytes=64)
            nc.vector.memset(tab_s[:].bitcast(I32), 0)
            nc.gpsimd.memset(w2_s_raw[:].rearrange("p a c -> p (a c)").bitcast(I32), 0)

            w1_rows = w1.rearrange("(p j) c -> p j c", j=PACK)
            w1_loaded = []
            for g in range(GROUPS):
                loaded = stage[g][:].rearrange("p (j c) -> p j c", j=PACK)
                nc.sync.dma_start(out=loaded, in_=w1_rows[:, :, g * PASS : (g + 1) * PASS])
                w1_loaded.append(loaded)
                if g == 0:
                    for quad in QUADRANTS:
                        nc.sync.dma_start(
                            out=tab_s[32 * quad : 32 * quad + 4, :].bitcast(I32),
                            in_=tab_scales[0, 4 * quad : 4 * quad + 4, :].bitcast(I32),
                        )
            nc.sync.dma_start(out=pick[:], in_=offs)
            tab_w = keep.tile([P, T], I32, name="tab_w", tag="tab_w", align_bytes=64)
            nc.sync.dma_start(out=tab_w[:], in_=tab_words[0].rearrange("p m t -> p (m t)").bitcast(I32))
            w2_raw = early.tile([P, GROUPS, 2 * H], U8, name="w2_raw", align_bytes=64)
            nc.sync.dma_start(out=w2_raw[:].bitcast(I32), in_=w2_words.rearrange("a p c -> p a c").bitcast(I32))
            for quad in QUADRANTS:
                nc.sync.dma_start(
                    out=w2_s_raw[32 * quad : 32 * quad + 4, :, :].bitcast(I32),
                    in_=w2_scales[:, 4 * quad : 4 * quad + 4, :].rearrange("a q c -> q a c").bitcast(I32),
                )
            nc.sync.dma_start(out=put[:], in_=offs2)

            gate = keep.tile([P, PACK, S], F32, name="gate", tag="gate", align_bytes=64)
            wgs_rows = wgs.rearrange("(q t) j -> q t j", t=PACK)

            def load_gate(u, first, count):
                rows, cols = slice(2 * u, 2 * u + 2), slice(first, first + count)
                for quad in QUADRANTS:
                    nc.sync.dma_start(out=gate[32 * quad : 32 * quad + 32, rows, cols], in_=wgs_rows[:, rows, cols])

            page0_rows = page0.rearrange("(g p t) m -> g t p m", p=P, t=PACK)
            out_1_rows = out_1.rearrange("(g p t) m -> g t p m", p=P, t=PACK)
            page = {}

            def load_pages(g, u):
                for t in (2 * u, 2 * u + 1):
                    page[g, t] = keep.tile([P, T2], F32, name="page%d%d" % (g, t))
                    nc.sync.dma_start(out=page[g, t][:], in_=page0_rows[g, t])

            load_gate(0, 0, QUARTER)
            load_pages(0, 0)
            load_gate(0, QUARTER, S - QUARTER)
            load_gate(1, 0, S)
            load_pages(0, 1)
            load_pages(1, 0)
            load_pages(1, 1)
            ident = keep.tile([P, P], F32, name="ident")
            make_identity(nc, ident[:])

            def quantise_weight(loaded, copy, rounded, codes, scales):
                copy(
                    out=rounded[:].rearrange("p (t m j) -> p m j t", t=PACK, j=PACK),
                    in_=loaded.rearrange("p j (m t) -> p m j t", t=PACK),
                )
                nc.vector.quantize_mx(out=codes.bitcast(FP8X4), scales=scales, in_=rounded[:])

            w1_c = early.tile([P, GROUPS, PASS], U32, name="w1_c", align_bytes=64)
            w1_s = early.tile([P, GROUPS, PASS], U8, name="w1_s", align_bytes=64)
            for g, copy in enumerate((nc.vector.tensor_copy, nc.scalar.copy)):
                w1_rounded = early.tile(
                    [P, PACK * PASS], BF16, name="w1_rounded", tag="w1_rounded", bufs=2, align_bytes=64
                )
                quantise_weight(w1_loaded[g], copy, w1_rounded, w1_c[:, g, :], w1_s[:, g, :])

            w4_loaded = []
            for g in range(GROUPS):
                loaded = stage[(2 + g) % 3][:].rearrange("p (j c) -> p j c", j=PACK)
                nc.sync.dma_start(
                    out=loaded, in_=w4[g * PASS : (g + 1) * PASS, :].rearrange("(p j) c -> p j c", j=PACK)
                )
                w4_loaded.append(loaded)
            nc.sync.dma_start(out=fetch[:], in_=offs3)
            bias = keep.tile([P, PACK], F32, name="bias")
            nc.sync.dma_start(out=bias[:], in_=b4.rearrange("(p t) -> p t", t=PACK))

            w2_c = early.tile([P, GROUPS, PACK, GROUPS, 2 * P], U8, name="w2_c", align_bytes=64)
            w2_s = early.tile([P, PACK, GROUPS, H // PACK], U8, name="w2_s", align_bytes=64)

            def deal_w2(g):
                nc.scalar.copy(
                    out=w2_c[:, g, :, :, :].bitcast(U16),
                    in_=w2_raw[:].bitcast(U16).rearrange("p a (g q t) -> p g t a q", g=GROUPS, t=PACK)[:, g, :, :, :],
                )

            deal_w2(0)

            v_c = early.tile([P, S], U32, name="v_c", align_bytes=64)
            v_s = early.tile([P, S], U8, name="v_s", align_bytes=64)

            def pick_scales(first, count):
                nc.vector.tensor_copy(v_s[:, first : first + count], tab_s[:].indirect(listed(pick, first, count)))

            def pick_words(first, count):
                nc.vector.tensor_copy(
                    v_c[:, first : first + count], tab_w[:].bitcast(U32).indirect(listed(pick, first, count))
                )

            pick_scales(0, S // 2)
            pick_words(0, QUARTER)
            nc.vector.tensor_copy(
                out=w2_s[:].rearrange("p t a q -> p t (a q)"),
                in_=w2_s_raw[:].rearrange("p a (q t) -> p t (a q)", t=PACK),
            )

            h = [keep.tile([P, PACK, S], F32, name="h%d" % g, tag="h%d" % g, align_bytes=64) for g in range(GROUPS)]
            raw_banks = {}
            mag_c = early.tile([P, CHUNKS, GROUPS * CHUNK], U32, name="mag_c", align_bytes=64)
            mag_s = early.tile([P, CHUNKS, GROUPS * CHUNK], U8, name="mag_s", align_bytes=64)

            def raw_pass(bank, c, g, t, start):
                cols = slice(c * CHUNK, (c + 1) * CHUNK)
                nc.tensor.matmul_mx(
                    out=bank[:, t * CHUNK : (t + 1) * CHUNK],
                    lhsT=w1_c[:, g, t * P : (t + 1) * P].bitcast(FP8X4),
                    lhsT_scale=w1_s[:, g, t * P : (t + 1) * P],
                    rhs=v_c[:, cols].bitcast(FP8X4),
                    rhs_scale=v_s[:, cols],
                    start=start,
                    stop=True,
                )

            def first_product(c):
                mag = early.tile([P, GROUPS, PASS], BF16, name="mag", bufs=2, align_bytes=64)
                for g in range(GROUPS):
                    bank = banks[c % 4] if g == 0 else banks[4 + c % 2]
                    for t in range(PACK):
                        raw_pass(bank, c, g, t, True)
                    nc.scalar.activation(
                        out=mag[:, g, :].rearrange("p (n t) -> p n t", t=PACK),
                        in_=bank[:].rearrange("p (t n) -> p n t", t=PACK),
                        func=ACT.Abs,
                    )
                    raw_banks[c, g] = bank
                nc.vector.quantize_mx(
                    out=mag_c[:, c, :].bitcast(FP8X4), scales=mag_s[:, c, :], in_=mag[:].rearrange("p g n -> p (g n)")
                )

            def mix_passes(bank, c, g, t, stop):
                for a in range(GROUPS):
                    nc.tensor.matmul_mx(
                        out=bank[:, t * CHUNK : (t + 1) * CHUNK],
                        lhsT=w2_c[:, g, t, a, :].bitcast(FP4X4),
                        lhsT_scale=w2_s[:, t, a, g * P : (g + 1) * P],
                        rhs=mag_c[:, c, a * CHUNK : (a + 1) * CHUNK].bitcast(FP8X4),
                        rhs_scale=mag_s[:, c, a * CHUNK : (a + 1) * CHUNK],
                        start=(a == 0),
                        stop=(stop and a == GROUPS - 1),
                    )

            def by_slice(columns):
                return columns.rearrange("p (t n) -> p t n", t=PACK)

            def h_chunk(c, g):
                return h[g][:, :, c * CHUNK : (c + 1) * CHUNK]

            def keep_raw(c, g, bufs):
                raw_sb = early.tile([P, BANK], F32, name="raw_sb%d" % g, bufs=bufs)
                nc.scalar.copy(out=raw_sb[:], in_=raw_banks[c, g][:])
                return raw_sb

            def add_on_vector(c, g, bank):
                raw_sb = keep_raw(c, g, 2)
                for t in range(PACK):
                    mix_passes(bank, c, g, t, True)
                nc.vector.tensor_tensor(out=h_chunk(c, g), in0=by_slice(bank[:]), in1=by_slice(raw_sb[:]), op=ADD)

            def add_by_repeat(c, g, bank):
                for t in range(PACK):
                    mix_passes(bank, c, g, t, False)
                    raw_pass(bank, c, g, t, False)
                nc.scalar.copy(out=h_chunk(c, g), in_=by_slice(bank[:]))

            def add_by_transposes(c, g, raw_sb, mixed, turned, back):
                staged = early.tile([P, 2, BANK], F32, name="staged", tag="w1_rounded", bufs=2, align_bytes=64)
                for t in range(PACK):
                    mix_passes(mixed, c, g, t, True)
                nc.scalar.copy(out=staged[:, 0, :], in_=mixed[:])
                for t in range(PACK):
                    cols = slice(t * P, (t + 1) * P)
                    for opens, term in ((True, staged[:, 0, cols]), (False, raw_sb[:, cols])):
                        nc.tensor.matmul(
                            turned[:, cols], lhsT=term, rhs=ident[:], is_transpose=True, start=opens, stop=not opens
                        )
                nc.scalar.copy(out=staged[:, 1, :], in_=turned[:])
                for t in range(PACK):
                    cols = slice(t * P, (t + 1) * P)
                    nc.tensor.transpose(back[:, cols], staged[:, 1, cols], ident[:])
                nc.scalar.copy(out=h_chunk(c, g), in_=by_slice(back[:]))

            def put_columns(g, t, first, count):
                nc.vector.tensor_tensor(
                    page[g, t][:].indirect(listed(put, first, count)),
                    h[g][:, t, first : first + count],
                    gate[:, t, first : first + count],
                    MULT,
                )

            first_product(0)
            first_product(1)
            pick_words(QUARTER, QUARTER)
            first_product(2)
            first_product(3)
            pick_scales(S // 2, S // 2)
            pick_words(S // 2, S // 2)
            raw_kept = {}
            for c in range(0, CHUNKS, 2):
                for chunk in (c, c + 1):
                    if chunk < ADDED_ON_VECTOR:
                        add_on_vector(chunk, 0, banks[6 + chunk % 2])
                    else:
                        add_by_repeat(chunk, 0, banks[6 + chunk % 2])
                for t in range(2):
                    put_columns(0, t, c * CHUNK, QUARTER)
                for chunk in (c + 2, c + 3):
                    if REPEATED <= chunk < CHUNKS:
                        raw_kept[chunk] = keep_raw(chunk, 1, CHUNKS - REPEATED)
                if c + 4 < CHUNKS:
                    first_product(c + 4)
                    first_product(c + 5)
            for t in range(2, PACK):
                put_columns(0, t, 0, S)
            deal_w2(1)
            for c in range(REPEATED, CHUNKS):
                add_by_transposes(c, 1, raw_kept[c], banks[c % 2], banks[2 + c % 2], banks[4 + c % 2])
            for c in range(REPEATED):
                add_by_repeat(c, 1, banks[6 + c % 2])
        late = ctx.enter_context(tc.tile_pool(name="late", bufs=4))

        def rounded_tile():
            return late.tile([P, PACK * BANK], BF16, name="rounded", bufs=8, align_bytes=64)

        w4_c = keep.tile([P, GROUPS, N], U32, name="w4_c", align_bytes=64)
        w4_s = keep.tile([P, GROUPS, N], U8, name="w4_s", align_bytes=64)
        for g in range(GROUPS):
            quantise_weight(w4_loaded[g], nc.scalar.copy, rounded_tile(), w4_c[:, g, :], w4_s[:, g, :])

        out_2_words = out_2.rearrange("g p m t -> g p (m t)")
        page_s = [keep.tile([P, T2], U8, name="page_s%d" % g, align_bytes=64) for g in range(GROUPS)]
        pairs = {}

        def turn_pair(g, u):
            pair = stage[(1 + 2 * g + u) % 3]
            halves = pair[:].bitcast(BF16).rearrange("m (b p e) -> m b p e", p=P, e=2)
            for two_blocks in range(T2 // (2 * P)):
                bank = banks[two_blocks]
                for b in range(2):
                    block = 2 * two_blocks + b
                    for e in range(2):
                        nc.tensor.transpose(
                            bank[:, (2 * b + e) * P : (2 * b + e + 1) * P],
                            page[g, 2 * u + e][:, block * P : (block + 1) * P],
                            ident[:],
                        )
                nc.scalar.copy(
                    out=halves[:, 2 * two_blocks : 2 * two_blocks + 2, :, :],
                    in_=bank[:].rearrange("m (b e p) -> m b p e", b=2, e=2),
                )
            pairs[g, u] = pair

        def store_pages(g, u):
            for e in range(2):
                nc.sync.dma_start(out=out_1_rows[g, 2 * u + e], in_=page[g, 2 * u + e][:])

        def turn_back(g):
            rounded_pieces = []
            for piece in range(T2 // BANK):
                rounded = rounded_tile()
                rounded_words = rounded[:].bitcast(F32)
                for half in range(2):
                    bank = banks[2 * piece + half]
                    for b in range(2):
                        block = 4 * piece + 2 * half + b
                        for u in range(2):
                            nc.tensor.transpose(
                                bank[:, (2 * b + u) * P : (2 * b + u + 1) * P],
                                pairs[g, u][:, block * P : (block + 1) * P],
                                ident[:],
                            )
                    nc.scalar.copy(
                        out=rounded_words[:, half * BANK : (half + 1) * BANK].rearrange(
                            "p (b m u) -> p b m u", b=2, u=2
                        ),
                        in_=bank[:].rearrange("p (b u m) -> p b m u", b=2, u=2),
                    )
                rounded_pieces.append(rounded)
            return rounded_pieces

        def page_words(g, rounded_pieces, first_piece, codes):
            for half in range(2):
                piece = first_piece + half
                nc.vector.quantize_mx(
                    out=codes[:, half * BANK : (half + 1) * BANK].bitcast(FP8X4),
                    scales=page_s[g][:, piece * BANK : (piece + 1) * BANK],
                    in_=rounded_pieces[piece][:],
                )
            nc.sync.dma_start(
                out=out_2_words[g, :, first_piece * PACK * BANK : (first_piece + 2) * PACK * BANK].bitcast(I32),
                in_=codes[:].bitcast(I32),
            )

        def page_scales(g):
            for quad in QUADRANTS:
                nc.sync.dma_start(
                    out=out_3[g, 4 * quad : 4 * quad + 4, :].bitcast(I32),
                    in_=page_s[g][32 * quad : 32 * quad + 4, :].bitcast(I32),
                )

        gm_rows = gm.rearrange("(g p t) j -> g p t j", p=P, t=PACK)
        factor = []
        for g, tag in enumerate(("tab_w", "h0")):
            factor.append(keep.tile([P, PACK, PICKS], F32, name="factor%d" % g, tag=tag, align_bytes=64))
            nc.sync.dma_start(out=factor[g][:], in_=gm_rows[g])

        for u in range(2):
            store_pages(0, u)
            turn_pair(0, u)
        for t in range(2):
            put_columns(1, t, 0, S)
        group_0_pieces = turn_back(0)
        for first_piece in (0, 2):
            codes_0 = late.tile([P, 2 * BANK], U32, name="page_c0", bufs=2, align_bytes=64)
            page_words(0, group_0_pieces, first_piece, codes_0)
        page_scales(0)
        store_pages(1, 0)
        turn_pair(1, 0)
        for t in range(2, PACK):
            put_columns(1, t, 0, S)
        store_pages(1, 1)
        turn_pair(1, 1)

        fetched = [
            keep.tile([P, GROUPS, PACK * BANK], F32, name="fetched%d" % b, tag=tag, align_bytes=64)
            for b, tag in enumerate(("gate", "h1"))
        ]
        out_0_rows = out_0.rearrange("(p t) j -> p t j", t=PACK)

        def fetch_columns(g, i):
            first, count = X_PIECES[i]
            values = fetched[i % 2][:, g, 0 : PACK * count]
            for t in range(PACK):
                looked_up = page[g, t][:].indirect(listed(fetch, first, count))
                nc.vector.tensor_tensor(
                    values[:, t * count : (t + 1) * count], looked_up, factor[g][:, t, first : first + count], MULT
                )
            if i == 0:
                x_rounded = pairs[0, 1][:].bitcast(BF16)[:, g * PACK * count : (g + 1) * PACK * count]
            else:
                label = "x%d%d" % (g, i)
                x_rounded = late.tile([P, PACK * count], BF16, name=label, tag=label, bufs=1, align_bytes=64)[:]
            nc.scalar.copy(
                out=x_rounded.rearrange("p (c n t) -> p c t n", n=4, t=PACK),
                in_=values.rearrange("p (t c n) -> p c t n", n=4, t=PACK),
            )
            x_c = ring.tile([P, BANK], U32, name="x_c", bufs=4, align_bytes=64)
            x_s = ring.tile([P, BANK], U8, name="x_s", bufs=4, align_bytes=64)
            nc.vector.quantize_mx(out=x_c[:, 0:count].bitcast(FP8X4), scales=x_s[:, 0:count], in_=x_rounded)
            return x_c, x_s

        def last_product(i, x_planes):
            first, count = X_PIECES[i]
            y = late.tile([P, PACK, count], F32, name="y%d" % i, bufs=1)
            for t in range(PACK):
                bank = banks[(PACK * i + t) % len(banks)]
                for g in range(GROUPS):
                    x_c, x_s = x_planes[g]
                    nc.tensor.matmul_mx(
                        out=bank[:, 0:count],
                        lhsT=w4_c[:, g, t * P : (t + 1) * P].bitcast(FP8X4),
                        lhsT_scale=w4_s[:, g, t * P : (t + 1) * P],
                        rhs=x_c[:, 0:count].bitcast(FP8X4),
                        rhs_scale=x_s[:, 0:count],
                        start=(g == 0),
                        stop=(g == GROUPS - 1),
                    )
                nc.scalar.activation(out=y[:, t, :], in_=bank[:, 0:count], func=ACT.Tanh, bias=bias[:, t : t + 1])
            nc.sync.dma_start(out=out_0_rows[:, :, first : first + count], in_=y[:])

        group_1_pieces = turn_back(1)
        x_pieces = {}
        for i in range(len(X_PIECES) + 1):
            if i < len(X_PIECES):
                x_pieces[i] = [fetch_columns(g, i) for g in range(GROUPS)]
            if i > 0:
                last_product(i - 1, x_pieces[i - 1])
        last_x = "x%d%d" % (GROUPS - 1, len(X_PIECES) - 1)
        codes_10 = keep.tile([P, 2 * BANK], U32, name="page_c10", tag="h0", align_bytes=64)
        page_words(1, group_1_pieces, 0, codes_10)
        codes_11 = late.tile([P, 2 * BANK], U32, name="page_c11", tag=last_x, bufs=1, align_bytes=64)
        page_words(1, group_1_pieces, 2, codes_11)
        page_scales(1)
